import numpy as np
import ml_dtypes


def mxq(x, axis, fmt="e4m3"):
    dtype, down = {"e4m3": (ml_dtypes.float8_e4m3fn, 7), "e5m2": (ml_dtypes.float8_e5m2, 14)}[fmt]
    v = np.moveaxis(np.asarray(x, np.float32).astype(ml_dtypes.bfloat16).astype(np.float64), axis, -1)
    blocks = v.reshape(v.shape[:-1] + (-1, 32))
    amax = np.abs(blocks).max(-1, keepdims=True)
    byte = np.maximum(np.where(amax > 0, np.frexp(amax)[1] - 1 + 127, 0) - down, 1)
    scale = np.exp2(byte - 127.0)
    codes = (blocks / scale).astype(np.float32).astype(dtype).astype(np.float64)
    return np.moveaxis((codes * scale).reshape(v.shape), -1, axis)


WIDE = False


def mx_kscale(k):
    if not WIDE:
        return np.ones(k)
    levels = np.array([24, -24, 12, -12, 0])
    if k % 512:
        return np.exp2(np.random.permutation(np.resize(levels, k // 32))).repeat(32)
    a = np.empty((k // 512, 16))
    for p in range(k // 512):
        a[p, :8] = np.random.permutation(np.resize(levels, 8))
        for g in range(8):
            far = levels[np.abs(levels - a[p, g]) >= 10]
            a[p, g + 8] = far[np.random.randint(len(far))]
    return np.exp2(a.ravel()).repeat(32)


def f64(x):
    return np.asarray(x).astype(np.float64)


def gelu(f):
    return 0.5 * f * (1.0 + np.tanh(np.sqrt(2.0 / np.pi) * (f + 0.044715 * f**3)))


K, N, T = 512, 512, 1024


def setup_inputs():
    n = np.random.standard_normal
    s = mx_kscale(K)[:, None]
    return {
        "w": (n((K, N)) / np.sqrt(K) / s).astype(np.float32),
        "x": (n((K, T)) * s).astype(np.float32),
        "b": (0.3 * n(N)).astype(np.float32),
    }


def reference(w, x, b):
    w_q_ = mxq(f64(w), 0, "e4m3")
    w_r_ = mxq(f64(w) - w_q_, 0, "e4m3")
    x_q_ = mxq(f64(x), 0, "e4m3")
    x_r_ = mxq(f64(x) - x_q_, 0, "e4m3")
    y = w_q_.T @ x_q_ + w_q_.T @ x_r_ + w_r_.T @ x_q_
    return gelu(y + f64(b)[:, None])

@@ -1,0 +1,222 @@
+from contextlib import ExitStack
+
+import concourse.mybir as mybir
+
+K, N, T = 512, 512, 1024
+FLOPS = 3 * 2 * K * N * T
+
+F32 = mybir.dt.float32
+BF16 = mybir.dt.bfloat16
+U32 = mybir.dt.uint32
+U8 = mybir.dt.uint8
+FP8X4 = mybir.dt.float8_e4m3fn_x4
+ALU = mybir.AluOpType
+ACT = mybir.ActivationFunctionType
+
+P = 128
+PACK = 4
+CH = 128
+RUN = 2
+BACK_BANKS = 2
+SUM_BANKS = 6
+PASS_COLUMNS = 1024
+
+
+def rows_view(ap):
+    return ap.rearrange("p j (c i) -> p c j i", i=RUN)
+
+
+def words_view(ap):
+    return ap.rearrange("p (c i j) -> p c j i", i=RUN, j=PACK)
+
+
+def tile_mix_tierb_three_gelu_kernel(tc, w, x, b, out):
+    nc = tc.nc
+    with ExitStack() as ctx:
+        sb = ctx.enter_context(tc.tile_pool(name="sb", bufs=1))
+        back_pool = ctx.enter_context(tc.psum_pool(name="back", bufs=BACK_BANKS))
+        sum_pool = ctx.enter_context(tc.psum_pool(name="sums", bufs=SUM_BANKS))
+        ctx.enter_context(tc.manual_schedule())
+
+        loads = [("w", 0, 1), ("w", 1, 1), ("x", 0, 2), ("w", 2, 2), ("x", 2, 2), ("x", 4, 2), ("x", 6, 2)]
+        src = {"w": w, "x": x}
+        raw = {}
+        order = []
+        for which, first, count in loads:
+            tile = sb.tile([P, PACK, count * CH], F32, name="raw_%s%d" % (which, first), align_bytes=64)
+            cols = src[which][:, first * CH : (first + count) * CH]
+            nc.sync.dma_start(out=tile[:], in_=cols.rearrange("(p j) c -> p j c", j=PACK))
+            for i in range(count):
+                raw[which, first + i] = tile[:, :, i * CH : (i + 1) * CH]
+                order.append((which, first + i))
+        bias = sb.tile([P, N // P], F32, name="bias", align_bytes=64)
+        with nc.allow_non_contiguous_dma(reason="one bias value a partition"):
+            nc.sync.dma_start(out=bias[:], in_=b.rearrange("(c p) -> p c", p=P))
+
+        ramp = sb.tile([P, K], BF16, name="ramp", align_bytes=64)
+        nc.gpsimd.iota(ramp[:], pattern=[[1, K]], base=0, channel_multiplier=-PACK, allow_small_or_imprecise_dtypes=True)
+        ident = sb.tile([P, PACK * K], BF16, name="ident", align_bytes=64)
+        for j in range(PACK):
+            nc.vector.tensor_scalar(
+                out=ident[:, j * K : (j + 1) * K], in0=ramp[:], scalar1=float(j), scalar2=None, op0=ALU.is_equal
+            )
+        id_codes = sb.tile([P, K], U32, name="id_codes", align_bytes=64)
+        id_scales = sb.tile([P, K], U8, name="id_scales", align_bytes=64)
+        nc.vector.quantize_mx(out=id_codes[:].bitcast(FP8X4), scales=id_scales[:], in_=ident[:])
+
+        codes = {}
+        scales = {}
+        for which, width in (("w", N), ("x", T)):
+            for tier in ("q", "r"):
+                codes[which, tier] = sb.tile([P, width], U32, name="codes_" + which + tier, align_bytes=64)
+                scales[which, tier] = sb.tile([P, width], U8, name="scales_" + which + tier, align_bytes=64)
+        rounded = {}
+        for which, width in (("w", N), ("x", T)):
+            for tier in ("q", "r"):
+                rounded[which, tier] = sb.tile([P, PACK * width], BF16, name="bf_" + which + tier, align_bytes=64)
+
+        done = set()
+
+        def bf_cols(which, tier, first, count):
+            return rounded[which, tier][:, first * CH * PACK : (first + count) * CH * PACK]
+
+        def cast(chunk, on_vector):
+            which, i = chunk
+            dst = words_view(bf_cols(which, "q", i, 1))
+            if on_vector:
+                nc.vector.tensor_copy(out=dst, in_=rows_view(raw[chunk]))
+            else:
+                nc.scalar.copy(out=dst, in_=rows_view(raw[chunk]))
+
+        def quantise(which, tier, first, count):
+            cols = slice(first * CH, (first + count) * CH)
+            nc.vector.quantize_mx(
+                out=codes[which, tier][:, cols].bitcast(FP8X4),
+                scales=scales[which, tier][:, cols],
+                in_=bf_cols(which, tier, first, count),
+            )
+            for i in range(first, first + count):
+                done.add((which, tier, i))
+
+        back = {}
+
+        def dequantise(chunk):
+            which, i = chunk
+            cols = slice(i * CH, (i + 1) * CH)
+            bank = back_pool.tile([P, PACK, CH], F32, name="back_bank")
+            for j in range(PACK):
+                nc.tensor.matmul_mx(
+                    out=bank[:, j, :],
+                    lhsT=id_codes[:, j * P : (j + 1) * P].bitcast(FP8X4),
+                    lhsT_scale=id_scales[:, j * P : (j + 1) * P],
+                    rhs=codes[which, "q"][:, cols].bitcast(FP8X4),
+                    rhs_scale=scales[which, "q"][:, cols],
+                    start=True,
+                    stop=True,
+                )
+            back[chunk] = bank
+
+        def leftover(chunk):
+            which, i = chunk
+            nc.vector.tensor_tensor(
+                out=words_view(bf_cols(which, "r", i, 1)),
+                in0=rows_view(raw[chunk]),
+                in1=rows_view(back[chunk][:]),
+                op=ALU.subtract,
+            )
+
+        banks = []
+        for first in (0, 2, 4):
+            banks.append((first, 2, (0, 1)))
+            banks.append((first, 2, (2, 3)))
+        banks.append((6, 1, (0, 1, 2, 3)))
+        banks.append((7, 1, (0, 1, 2, 3)))
+        waiting = []
+        for n, (first, count, tiles) in enumerate(banks):
+            for w_tier, x_tier in (("q", "q"), ("r", "q"), ("q", "r")):
+                for c in tiles:
+                    waiting.append((n, c, w_tier, x_tier))
+        sums = {}
+        left = [3 * len(tiles) for first, count, tiles in banks]
+        closed = []
+        emptied = set()
+
+        def ready(item):
+            n, c, w_tier, x_tier = item
+            first, count, tiles = banks[n]
+            if n >= SUM_BANKS and (n - SUM_BANKS) not in emptied:
+                return False
+            if n > 0 and n not in sums and (n - 1) not in sums:
+                return False
+            return ("w", w_tier, c) in done and all(("x", x_tier, i) in done for i in range(first, first + count))
+
+        def multiply(budget):
+            for item in list(waiting):
+                if budget <= 0:
+                    break
+                if not ready(item):
+                    continue
+                n, c, w_tier, x_tier = item
+                first, count, tiles = banks[n]
+                opening = n not in sums
+                if opening:
+                    sums[n] = sum_pool.tile([P, len(tiles), count * CH], F32, name="sum_bank")
+                left[n] = left[n] - 1
+                w_cols = slice(c * P, (c + 1) * P)
+                x_cols = slice(first * CH, (first + count) * CH)
+                nc.tensor.matmul_mx(
+                    out=sums[n][:, tiles.index(c), :],
+                    lhsT=codes["w", w_tier][:, w_cols].bitcast(FP8X4),
+                    lhsT_scale=scales["w", w_tier][:, w_cols],
+                    rhs=codes["x", x_tier][:, x_cols].bitcast(FP8X4),
+                    rhs_scale=scales["x", x_tier][:, x_cols],
+                    start=opening,
+                    stop=left[n] == 0,
+                )
+                waiting.remove(item)
+                budget = budget - count * CH
+                if left[n] == 0:
+                    closed.append(n)
+
+        out_rows = out.rearrange("(c p) t -> p c t", p=P)
+
+        def finish():
+            for n in list(closed):
+                first, count, tiles = banks[n]
+                result = sb.tile([P, len(tiles), count * CH], F32, name="result%d" % n, align_bytes=64)
+                for s, c in enumerate(tiles):
+                    nc.scalar.activation(
+                        out=result[:, s, :], in_=sums[n][:, s, :], func=ACT.Gelu_apprx_tanh, bias=bias[:, c : c + 1]
+                    )
+                nc.sync.dma_start(
+                    out=out_rows[:, tiles[0] : tiles[-1] + 1, first * CH : (first + count) * CH], in_=result[:]
+                )
+                closed.remove(n)
+                emptied.add(n)
+
+        last = len(order) - 1
+        for s in range(2):
+            cast(order[s], s == 1)
+            quantise(order[s][0], "q", order[s][1], 1)
+            dequantise(order[s])
+        ahead = 2
+        for s in range(len(order)):
+            leftover(order[s])
+            if s > 0:
+                quantise(order[s - 1][0], "r", order[s - 1][1], 1)
+            if ahead <= last:
+                count = 1 if s < 4 else 2
+                for i in range(count):
+                    cast(order[ahead + i], False)
+                quantise(order[ahead][0], "q", order[ahead][1], count)
+                ahead = ahead + count
+            if s + 2 <= last:
+                dequantise(order[s + 2])
+            if ahead > last:
+                finish()
+            multiply(PASS_COLUMNS if s + 2 <= last else 4 * PASS_COLUMNS)
+        finish()
+        quantise(order[last][0], "r", order[last][1], 1)
+        multiply(4 * PASS_COLUMNS)
+        finish()
+        assert not waiting

@@ -17,8 +17,8 @@ P = 128
 PACK = 4
 CH = 128
 RUN = 2
-BACK_BANKS = 2
-SUM_BANKS = 6
+BACK_BANKS = 3
+SUM_BANKS = 5
 PASS_COLUMNS = 1024
 
 
@@ -36,7 +36,7 @@ def tile_mix_tierb_three_gelu_kernel(tc, w, x, b, out):
         sb = ctx.enter_context(tc.tile_pool(name="sb", bufs=1))
         back_pool = ctx.enter_context(tc.psum_pool(name="back", bufs=BACK_BANKS))
         sum_pool = ctx.enter_context(tc.psum_pool(name="sums", bufs=SUM_BANKS))
-        ctx.enter_context(tc.manual_schedule())
+        ctx.enter_context(tc.manual_schedule(engines={mybir.EngineType.DVE, mybir.EngineType.SP}))
 
         loads = [("w", 0, 1), ("w", 1, 1), ("x", 0, 2), ("w", 2, 2), ("x", 2, 2), ("x", 4, 2), ("x", 6, 2)]
         src = {"w": w, "x": x}
@@ -52,6 +52,10 @@ def tile_mix_tierb_three_gelu_kernel(tc, w, x, b, out):
         bias = sb.tile([P, N // P], F32, name="bias", align_bytes=64)
         with nc.allow_non_contiguous_dma(reason="one bias value a partition"):
             nc.sync.dma_start(out=bias[:], in_=b.rearrange("(c p) -> p c", p=P))
+
+        warm = sb.tile([P, 2], F32, name="warm", align_bytes=64)
+        nc.vector.memset(warm[:, 0:1], 0.0)
+        nc.scalar.activation(out=warm[:, 1:2], in_=warm[:, 0:1], func=ACT.Gelu_apprx_tanh)
 
         ramp = sb.tile([P, K], BF16, name="ramp", align_bytes=64)
         nc.gpsimd.iota(ramp[:], pattern=[[1, K]], base=0, channel_multiplier=-PACK, allow_small_or_imprecise_dtypes=True)
@@ -80,13 +84,16 @@ def tile_mix_tierb_three_gelu_kernel(tc, w, x, b, out):
         def bf_cols(which, tier, first, count):
             return rounded[which, tier][:, first * CH * PACK : (first + count) * CH * PACK]
 
-        def cast(chunk, on_vector):
+        def cast(chunk, shared):
             which, i = chunk
             dst = words_view(bf_cols(which, "q", i, 1))
-            if on_vector:
-                nc.vector.tensor_copy(out=dst, in_=rows_view(raw[chunk]))
+            rows = rows_view(raw[chunk])
+            if shared:
+                half = CH // RUN // 2
+                nc.scalar.copy(out=dst[:, :half], in_=rows[:, :half])
+                nc.vector.tensor_copy(out=dst[:, half:], in_=rows[:, half:])
             else:
-                nc.scalar.copy(out=dst, in_=rows_view(raw[chunk]))
+                nc.scalar.copy(out=dst, in_=rows)
 
         def quantise(which, tier, first, count):
             cols = slice(first * CH, (first + count) * CH)
@@ -188,34 +195,35 @@ def tile_mix_tierb_three_gelu_kernel(tc, w, x, b, out):
                     nc.scalar.activation(
                         out=result[:, s, :], in_=sums[n][:, s, :], func=ACT.Gelu_apprx_tanh, bias=bias[:, c : c + 1]
                     )
-                nc.sync.dma_start(
-                    out=out_rows[:, tiles[0] : tiles[-1] + 1, first * CH : (first + count) * CH], in_=result[:]
-                )
+                    if s % 2 == 1:
+                        nc.sync.dma_start(
+                            out=out_rows[:, c - 1 : c + 1, first * CH : (first + count) * CH],
+                            in_=result[:, s - 1 : s + 1, :],
+                        )
                 closed.remove(n)
                 emptied.add(n)
 
         last = len(order) - 1
         for s in range(2):
-            cast(order[s], s == 1)
+            cast(order[s], s == 0)
             quantise(order[s][0], "q", order[s][1], 1)
             dequantise(order[s])
-        ahead = 2
+        quantised = 2
+        returned = 2
         for s in range(len(order)):
             leftover(order[s])
+            while quantised <= min(last, 2 + (3 * s + 1) // 2):
+                cast(order[quantised], False)
+                quantise(order[quantised][0], "q", order[quantised][1], 1)
+                quantised = quantised + 1
             if s > 0:
                 quantise(order[s - 1][0], "r", order[s - 1][1], 1)
-            if ahead <= last:
-                count = 1 if s < 4 else 2
-                for i in range(count):
-                    cast(order[ahead + i], False)
-                quantise(order[ahead][0], "q", order[ahead][1], count)
-                ahead = ahead + count
-            if s + 2 <= last:
-                dequantise(order[s + 2])
-            if ahead > last:
-                finish()
-            multiply(PASS_COLUMNS if s + 2 <= last else 4 * PASS_COLUMNS)
-        finish()
+            while returned <= min(quantised - 1, s + BACK_BANKS):
+                dequantise(order[returned])
+                returned = returned + 1
+            multiply(16 * PASS_COLUMNS)
+            finish()
+            multiply(16 * PASS_COLUMNS)
         quantise(order[last][0], "r", order[last][1], 1)
         multiply(4 * PASS_COLUMNS)
         finish()

@@ -19,7 +19,12 @@ CH = 128
 RUN = 2
 BACK_BANKS = 3
 SUM_BANKS = 5
-PASS_COLUMNS = 1024
+AHEAD = 3
+REOPEN = 1
+BUDGET = 768
+ORD = "dcm"
+QN, QD = 3, 2
+WARM_PASSES = 20
 
 
 def rows_view(ap):
@@ -36,9 +41,9 @@ def tile_mix_tierb_three_gelu_kernel(tc, w, x, b, out):
         sb = ctx.enter_context(tc.tile_pool(name="sb", bufs=1))
         back_pool = ctx.enter_context(tc.psum_pool(name="back", bufs=BACK_BANKS))
         sum_pool = ctx.enter_context(tc.psum_pool(name="sums", bufs=SUM_BANKS))
-        ctx.enter_context(tc.manual_schedule(engines={mybir.EngineType.DVE, mybir.EngineType.SP}))
+        ctx.enter_context(tc.manual_schedule())
 
-        loads = [("w", 0, 1), ("w", 1, 1), ("x", 0, 2), ("w", 2, 2), ("x", 2, 2), ("x", 4, 2), ("x", 6, 2)]
+        loads = [("w", 0, 1), ("x", 0, 1), ("x", 1, 1), ("x", 2, 2), ("w", 1, 1), ("w", 2, 2), ("x", 4, 2), ("x", 6, 2)]
         src = {"w": w, "x": x}
         raw = {}
         order = []
@@ -56,6 +61,23 @@ def tile_mix_tierb_three_gelu_kernel(tc, w, x, b, out):
         warm = sb.tile([P, 2], F32, name="warm", align_bytes=64)
         nc.vector.memset(warm[:, 0:1], 0.0)
         nc.scalar.activation(out=warm[:, 1:2], in_=warm[:, 0:1], func=ACT.Gelu_apprx_tanh)
+
+        warm_in = sb.tile([P, PACK * CH], BF16, name="warm_in", align_bytes=64)
+        warm_codes = sb.tile([P, CH], U32, name="warm_codes", align_bytes=64)
+        warm_scales = sb.tile([P, CH], U8, name="warm_scales", align_bytes=64)
+        nc.vector.memset(warm_in[:], 1.0)
+        nc.vector.quantize_mx(out=warm_codes[:].bitcast(FP8X4), scales=warm_scales[:], in_=warm_in[:])
+        warm_bank = sum_pool.tile([P, PACK, CH], F32, name="sum_bank")
+        for j in range(WARM_PASSES):
+            nc.tensor.matmul_mx(
+                out=warm_bank[:, j % PACK, :],
+                lhsT=warm_codes[:].bitcast(FP8X4),
+                lhsT_scale=warm_scales[:],
+                rhs=warm_codes[:].bitcast(FP8X4),
+                rhs_scale=warm_scales[:],
+                start=True,
+                stop=True,
+            )
 
         ramp = sb.tile([P, K], BF16, name="ramp", align_bytes=64)
         nc.gpsimd.iota(ramp[:], pattern=[[1, K]], base=0, channel_multiplier=-PACK, allow_small_or_imprecise_dtypes=True)
@@ -132,99 +154,86 @@ def tile_mix_tierb_three_gelu_kernel(tc, w, x, b, out):
                 op=ALU.subtract,
             )
 
-        banks = []
-        for first in (0, 2, 4):
-            banks.append((first, 2, (0, 1)))
-            banks.append((first, 2, (2, 3)))
-        banks.append((6, 1, (0, 1, 2, 3)))
-        banks.append((7, 1, (0, 1, 2, 3)))
-        waiting = []
-        for n, (first, count, tiles) in enumerate(banks):
-            for w_tier, x_tier in (("q", "q"), ("r", "q"), ("q", "r")):
-                for c in tiles:
-                    waiting.append((n, c, w_tier, x_tier))
+        n_tiles = N // P
+        half = T // CH // 2
+        blocks = [(0, half, (c,)) for c in range(n_tiles)]
+        blocks = blocks + [(i, 1, tuple(range(n_tiles))) for i in range(half, 2 * half)]
         sums = {}
-        left = [3 * len(tiles) for first, count, tiles in banks]
-        closed = []
-        emptied = set()
-
-        def ready(item):
-            n, c, w_tier, x_tier = item
-            first, count, tiles = banks[n]
-            if n >= SUM_BANKS and (n - SUM_BANKS) not in emptied:
-                return False
-            if n > 0 and n not in sums and (n - 1) not in sums:
-                return False
-            return ("w", w_tier, c) in done and all(("x", x_tier, i) in done for i in range(first, first + count))
-
-        def multiply(budget):
-            for item in list(waiting):
-                if budget <= 0:
-                    break
-                if not ready(item):
-                    continue
-                n, c, w_tier, x_tier = item
-                first, count, tiles = banks[n]
-                opening = n not in sums
-                if opening:
-                    sums[n] = sum_pool.tile([P, len(tiles), count * CH], F32, name="sum_bank")
-                left[n] = left[n] - 1
-                w_cols = slice(c * P, (c + 1) * P)
-                x_cols = slice(first * CH, (first + count) * CH)
-                nc.tensor.matmul_mx(
-                    out=sums[n][:, tiles.index(c), :],
-                    lhsT=codes["w", w_tier][:, w_cols].bitcast(FP8X4),
-                    lhsT_scale=scales["w", w_tier][:, w_cols],
-                    rhs=codes["x", x_tier][:, x_cols].bitcast(FP8X4),
-                    rhs_scale=scales["x", x_tier][:, x_cols],
-                    start=opening,
-                    stop=left[n] == 0,
-                )
-                waiting.remove(item)
-                budget = budget - count * CH
-                if left[n] == 0:
-                    closed.append(n)
-
         out_rows = out.rearrange("(c p) t -> p c t", p=P)
 
-        def finish():
-            for n in list(closed):
-                first, count, tiles = banks[n]
-                result = sb.tile([P, len(tiles), count * CH], F32, name="result%d" % n, align_bytes=64)
-                for s, c in enumerate(tiles):
-                    nc.scalar.activation(
-                        out=result[:, s, :], in_=sums[n][:, s, :], func=ACT.Gelu_apprx_tanh, bias=bias[:, c : c + 1]
+        waiting = [
+            (n, s, w_tier, x_tier)
+            for n, (first, count, tiles) in enumerate(blocks)
+            for w_tier, x_tier in (("q", "q"), ("r", "q"), ("q", "r"))
+            for s in range(len(tiles))
+        ]
+
+        def ready(n, s, w_tier, x_tier):
+            first, count, tiles = blocks[n]
+            return ("w", w_tier, tiles[s]) in done and all(
+                ("x", x_tier, i) in done for i in range(first, first + count)
+            )
+
+        def multiply(columns, lowest, highest):
+            for n, s, w_tier, x_tier in list(waiting):
+                if columns > 0 and lowest <= n <= highest and ready(n, s, w_tier, x_tier):
+                    first, count, tiles = blocks[n]
+                    opening = n not in sums
+                    if opening:
+                        sums[n] = sum_pool.tile([P, len(tiles), count * CH], F32, name="sum_bank")
+                    waiting.remove((n, s, w_tier, x_tier))
+                    w_cols = slice(tiles[s] * P, (tiles[s] + 1) * P)
+                    x_cols = slice(first * CH, (first + count) * CH)
+                    nc.tensor.matmul_mx(
+                        out=sums[n][:, s, :],
+                        lhsT=codes["w", w_tier][:, w_cols].bitcast(FP8X4),
+                        lhsT_scale=scales["w", w_tier][:, w_cols],
+                        rhs=codes["x", x_tier][:, x_cols].bitcast(FP8X4),
+                        rhs_scale=scales["x", x_tier][:, x_cols],
+                        start=opening,
+                        stop=all(item[0] != n for item in waiting),
                     )
-                    if s % 2 == 1:
-                        nc.sync.dma_start(
-                            out=out_rows[:, c - 1 : c + 1, first * CH : (first + count) * CH],
-                            in_=result[:, s - 1 : s + 1, :],
-                        )
-                closed.remove(n)
-                emptied.add(n)
+                    columns = columns - count * CH
+
+        def finish(n):
+            first, count, tiles = blocks[n]
+            result = sb.tile([P, len(tiles), count * CH], F32, name="result%d" % n, align_bytes=64)
+            together = min(2, len(tiles))
+            for s, c in enumerate(tiles):
+                nc.scalar.activation(
+                    out=result[:, s, :], in_=sums[n][:, s, :], func=ACT.Gelu_apprx_tanh, bias=bias[:, c : c + 1]
+                )
+                if (s + 1) % together == 0:
+                    nc.sync.dma_start(
+                        out=out_rows[:, c + 1 - together : c + 1, first * CH : (first + count) * CH],
+                        in_=result[:, s + 1 - together : s + 1, :],
+                    )
 
         last = len(order) - 1
-        for s in range(2):
+        for s in range(len(order)):
             cast(order[s], s == 0)
-            quantise(order[s][0], "q", order[s][1], 1)
-            dequantise(order[s])
+            if s < 2:
+                quantise(order[s][0], "q", order[s][1], 1)
+                dequantise(order[s])
         quantised = 2
         returned = 2
-        for s in range(len(order)):
-            leftover(order[s])
-            while quantised <= min(last, 2 + (3 * s + 1) // 2):
-                cast(order[quantised], False)
-                quantise(order[quantised][0], "q", order[quantised][1], 1)
-                quantised = quantised + 1
+        for s in range(len(order) + 1):
+            if s <= last:
+                leftover(order[s])
             if s > 0:
                 quantise(order[s - 1][0], "r", order[s - 1][1], 1)
-            while returned <= min(quantised - 1, s + BACK_BANKS):
-                dequantise(order[returned])
-                returned = returned + 1
-            multiply(16 * PASS_COLUMNS)
-            finish()
-            multiply(16 * PASS_COLUMNS)
-        quantise(order[last][0], "r", order[last][1], 1)
-        multiply(4 * PASS_COLUMNS)
-        finish()
+            while quantised <= min(last, 2 + (QN * s) // QD):
+                quantise(order[quantised][0], "q", order[quantised][1], 1)
+                quantised = quantised + 1
+            closing = s - 1 - half
+            for what in ORD:
+                if what == "c" and closing >= 0:
+                    multiply(K * N, closing, closing)
+                    finish(closing)
+                if what == "d":
+                    while returned <= min(quantised - 1, s + AHEAD):
+                        dequantise(order[returned])
+                        returned = returned + 1
+                if what == "m":
+                    multiply(BUDGET, 0, max(closing - REOPEN, -1) + SUM_BANKS)
         assert not waiting

@@ -16,7 +16,7 @@ ACT = mybir.ActivationFunctionType
 P = 128
 PACK = 4
 CH = 128
-RUN = 2
+RUN = 4
 BACK_BANKS = 3
 SUM_BANKS = 5
 AHEAD = 3

@@ -11,84 +11,73 @@ U32 = mybir.dt.uint32
 U8 = mybir.dt.uint8
 FP8X4 = mybir.dt.float8_e4m3fn_x4
 ALU = mybir.AluOpType
-ACT = mybir.ActivationFunctionType
+GELU = mybir.ActivationFunctionType.Gelu_apprx_tanh
 
 P = 128
 PACK = 4
-CH = 128
+CHUNK = 128
 RUN = 4
 BACK_BANKS = 3
 SUM_BANKS = 5
-AHEAD = 3
-REOPEN = 1
-BUDGET = 768
-ORD = "dcm"
-QN, QD = 3, 2
-WARM_PASSES = 20
+PASS_CHUNKS = 2
+STORE_TILES = 2
+FILL_BEFORE_FIRST_BLOCK = 1024
+FILL_AFTER_FIRST_BLOCK = 640
 
 
-def rows_view(ap):
-    return ap.rearrange("p j (c i) -> p c j i", i=RUN)
+def rows_view(rows):
+    return rows.rearrange("p j (g i) -> p g j i", i=RUN)
 
 
-def words_view(ap):
-    return ap.rearrange("p (c i j) -> p c j i", i=RUN, j=PACK)
+def words_view(interleaved):
+    return interleaved.rearrange("p (g i j) -> p g j i", i=RUN, j=PACK)
 
 
 def tile_mix_tierb_three_gelu_kernel(tc, w, x, b, out):
     nc = tc.nc
+    n_tiles = N // P
+    x_chunks = T // CHUNK
+    half = x_chunks // 2
+
     with ExitStack() as ctx:
         sb = ctx.enter_context(tc.tile_pool(name="sb", bufs=1))
         back_pool = ctx.enter_context(tc.psum_pool(name="back", bufs=BACK_BANKS))
         sum_pool = ctx.enter_context(tc.psum_pool(name="sums", bufs=SUM_BANKS))
         ctx.enter_context(tc.manual_schedule())
 
-        loads = [("w", 0, 1), ("x", 0, 1), ("x", 1, 1), ("x", 2, 2), ("w", 1, 1), ("w", 2, 2), ("x", 4, 2), ("x", 6, 2)]
-        src = {"w": w, "x": x}
+        loads = [("w", 0, 1), ("w", 1, 1)]
+        loads = loads + [("x", i, 2) for i in range(0, half, 2)] + [("w", 2, 2)]
+        loads = loads + [("x", i, 2) for i in range(half, x_chunks, 2)]
+        matrix = {"w": w, "x": x}
         raw = {}
         order = []
         for which, first, count in loads:
-            tile = sb.tile([P, PACK, count * CH], F32, name="raw_%s%d" % (which, first), align_bytes=64)
-            cols = src[which][:, first * CH : (first + count) * CH]
-            nc.sync.dma_start(out=tile[:], in_=cols.rearrange("(p j) c -> p j c", j=PACK))
+            landed = sb.tile([P, PACK, count * CHUNK], F32, name="raw_%s%d" % (which, first), align_bytes=64)
+            columns = matrix[which][:, first * CHUNK : (first + count) * CHUNK]
+            nc.sync.dma_start(out=landed[:], in_=columns.rearrange("(p j) c -> p j c", j=PACK))
             for i in range(count):
-                raw[which, first + i] = tile[:, :, i * CH : (i + 1) * CH]
+                raw[which, first + i] = landed[:, :, i * CHUNK : (i + 1) * CHUNK]
                 order.append((which, first + i))
-        bias = sb.tile([P, N // P], F32, name="bias", align_bytes=64)
-        with nc.allow_non_contiguous_dma(reason="one bias value a partition"):
+        bias = sb.tile([P, n_tiles], F32, name="bias", align_bytes=64)
+        with nc.allow_non_contiguous_dma(reason="one bias value for each partition and n tile"):
             nc.sync.dma_start(out=bias[:], in_=b.rearrange("(c p) -> p c", p=P))
 
-        warm = sb.tile([P, 2], F32, name="warm", align_bytes=64)
-        nc.vector.memset(warm[:, 0:1], 0.0)
-        nc.scalar.activation(out=warm[:, 1:2], in_=warm[:, 0:1], func=ACT.Gelu_apprx_tanh)
-
-        warm_in = sb.tile([P, PACK * CH], BF16, name="warm_in", align_bytes=64)
-        warm_codes = sb.tile([P, CH], U32, name="warm_codes", align_bytes=64)
-        warm_scales = sb.tile([P, CH], U8, name="warm_scales", align_bytes=64)
-        nc.vector.memset(warm_in[:], 1.0)
-        nc.vector.quantize_mx(out=warm_codes[:].bitcast(FP8X4), scales=warm_scales[:], in_=warm_in[:])
-        warm_bank = sum_pool.tile([P, PACK, CH], F32, name="sum_bank")
-        for j in range(WARM_PASSES):
-            nc.tensor.matmul_mx(
-                out=warm_bank[:, j % PACK, :],
-                lhsT=warm_codes[:].bitcast(FP8X4),
-                lhsT_scale=warm_scales[:],
-                rhs=warm_codes[:].bitcast(FP8X4),
-                rhs_scale=warm_scales[:],
-                start=True,
-                stop=True,
-            )
+        table_warm = sb.tile([P, 2], F32, name="table_warm", align_bytes=64)
+        nc.vector.memset(table_warm[:, 0:1], 0.0)
+        nc.scalar.activation(out=table_warm[:, 1:2], in_=table_warm[:, 0:1], func=GELU)
 
         ramp = sb.tile([P, K], BF16, name="ramp", align_bytes=64)
-        nc.gpsimd.iota(ramp[:], pattern=[[1, K]], base=0, channel_multiplier=-PACK, allow_small_or_imprecise_dtypes=True)
-        ident = sb.tile([P, PACK * K], BF16, name="ident", align_bytes=64)
+        nc.gpsimd.iota(
+            ramp[:], pattern=[[1, K]], base=0, channel_multiplier=-PACK, allow_small_or_imprecise_dtypes=True
+        )
+        identity = sb.tile([P, PACK * K], BF16, name="identity", align_bytes=64)
         for j in range(PACK):
             nc.vector.tensor_scalar(
-                out=ident[:, j * K : (j + 1) * K], in0=ramp[:], scalar1=float(j), scalar2=None, op0=ALU.is_equal
+                out=identity[:, j * K : (j + 1) * K], in0=ramp[:], scalar1=float(j), scalar2=None, op0=ALU.is_equal
             )
         id_codes = sb.tile([P, K], U32, name="id_codes", align_bytes=64)
         id_scales = sb.tile([P, K], U8, name="id_scales", align_bytes=64)
-        nc.vector.quantize_mx(out=id_codes[:].bitcast(FP8X4), scales=id_scales[:], in_=ident[:])
+        nc.vector.quantize_mx(out=id_codes[:].bitcast(FP8X4), scales=id_scales[:], in_=identity[:])
 
         codes = {}
         scales = {}
@@ -100,140 +89,136 @@ def tile_mix_tierb_three_gelu_kernel(tc, w, x, b, out):
         for which, width in (("w", N), ("x", T)):
             for tier in ("q", "r"):
                 rounded[which, tier] = sb.tile([P, PACK * width], BF16, name="bf_" + which + tier, align_bytes=64)
-
-        done = set()
-
-        def bf_cols(which, tier, first, count):
-            return rounded[which, tier][:, first * CH * PACK : (first + count) * CH * PACK]
-
-        def cast(chunk, shared):
-            which, i = chunk
-            dst = words_view(bf_cols(which, "q", i, 1))
-            rows = rows_view(raw[chunk])
-            if shared:
-                half = CH // RUN // 2
-                nc.scalar.copy(out=dst[:, :half], in_=rows[:, :half])
-                nc.vector.tensor_copy(out=dst[:, half:], in_=rows[:, half:])
-            else:
-                nc.scalar.copy(out=dst, in_=rows)
-
-        def quantise(which, tier, first, count):
-            cols = slice(first * CH, (first + count) * CH)
-            nc.vector.quantize_mx(
-                out=codes[which, tier][:, cols].bitcast(FP8X4),
-                scales=scales[which, tier][:, cols],
-                in_=bf_cols(which, tier, first, count),
-            )
-            for i in range(first, first + count):
-                done.add((which, tier, i))
-
+        quantised = set()
         back = {}
 
-        def dequantise(chunk):
+        def rounded_chunk(chunk, tier):
             which, i = chunk
-            cols = slice(i * CH, (i + 1) * CH)
-            bank = back_pool.tile([P, PACK, CH], F32, name="back_bank")
+            return rounded[which, tier][:, i * CHUNK * PACK : (i + 1) * CHUNK * PACK]
+
+        def round_and_interleave(chunk, shared):
+            words = words_view(rounded_chunk(chunk, "q"))
+            rows = rows_view(raw[chunk])
+            if shared:
+                cut = CHUNK // RUN // 2
+                nc.scalar.copy(out=words[:, :cut], in_=rows[:, :cut])
+                nc.vector.tensor_copy(out=words[:, cut:], in_=rows[:, cut:])
+            else:
+                nc.scalar.copy(out=words, in_=rows)
+
+        def quantise(chunk, tier):
+            which, i = chunk
+            columns = slice(i * CHUNK, (i + 1) * CHUNK)
+            nc.vector.quantize_mx(
+                out=codes[which, tier][:, columns].bitcast(FP8X4),
+                scales=scales[which, tier][:, columns],
+                in_=rounded_chunk(chunk, tier),
+            )
+            quantised.add((which, tier, i))
+
+        def bring_back(chunk):
+            which, i = chunk
+            columns = slice(i * CHUNK, (i + 1) * CHUNK)
+            back[chunk] = back_pool.tile([P, PACK, CHUNK], F32, name="back_bank")
             for j in range(PACK):
                 nc.tensor.matmul_mx(
-                    out=bank[:, j, :],
+                    out=back[chunk][:, j, :],
                     lhsT=id_codes[:, j * P : (j + 1) * P].bitcast(FP8X4),
                     lhsT_scale=id_scales[:, j * P : (j + 1) * P],
-                    rhs=codes[which, "q"][:, cols].bitcast(FP8X4),
-                    rhs_scale=scales[which, "q"][:, cols],
+                    rhs=codes[which, "q"][:, columns].bitcast(FP8X4),
+                    rhs_scale=scales[which, "q"][:, columns],
                     start=True,
                     stop=True,
                 )
-            back[chunk] = bank
 
-        def leftover(chunk):
-            which, i = chunk
+        def subtract(chunk):
             nc.vector.tensor_tensor(
-                out=words_view(bf_cols(which, "r", i, 1)),
+                out=words_view(rounded_chunk(chunk, "r")),
                 in0=rows_view(raw[chunk]),
                 in1=rows_view(back[chunk][:]),
                 op=ALU.subtract,
             )
 
-        n_tiles = N // P
-        half = T // CH // 2
         blocks = [(0, half, (c,)) for c in range(n_tiles)]
-        blocks = blocks + [(i, 1, tuple(range(n_tiles))) for i in range(half, 2 * half)]
+        blocks = blocks + [(i, 1, tuple(range(n_tiles))) for i in range(half, x_chunks)]
+        waiting = [
+            (block, place, part, w_tier, x_tier)
+            for block, (first, count, tiles) in enumerate(blocks)
+            for w_tier, x_tier in (("q", "q"), ("r", "q"), ("q", "r"))
+            for place in range(len(tiles))
+            for part in range(0, count, PASS_CHUNKS)
+        ]
         sums = {}
         out_rows = out.rearrange("(c p) t -> p c t", p=P)
 
-        waiting = [
-            (n, s, w_tier, x_tier)
-            for n, (first, count, tiles) in enumerate(blocks)
-            for w_tier, x_tier in (("q", "q"), ("r", "q"), ("q", "r"))
-            for s in range(len(tiles))
-        ]
+        def ready(block, place, part, w_tier, x_tier):
+            first, count, tiles = blocks[block]
+            needed = range(first + part, first + min(part + PASS_CHUNKS, count))
+            return ("w", w_tier, tiles[place]) in quantised and all(("x", x_tier, i) in quantised for i in needed)
 
-        def ready(n, s, w_tier, x_tier):
-            first, count, tiles = blocks[n]
-            return ("w", w_tier, tiles[s]) in done and all(
-                ("x", x_tier, i) in done for i in range(first, first + count)
-            )
-
-        def multiply(columns, lowest, highest):
-            for n, s, w_tier, x_tier in list(waiting):
-                if columns > 0 and lowest <= n <= highest and ready(n, s, w_tier, x_tier):
-                    first, count, tiles = blocks[n]
-                    opening = n not in sums
+        def multiply(budget, lowest, highest):
+            for item in list(waiting):
+                block, place, part, w_tier, x_tier = item
+                if budget > 0 and lowest <= block <= highest and ready(*item):
+                    first, count, tiles = blocks[block]
+                    width = min(PASS_CHUNKS, count) * CHUNK
+                    opening = block not in sums
                     if opening:
-                        sums[n] = sum_pool.tile([P, len(tiles), count * CH], F32, name="sum_bank")
-                    waiting.remove((n, s, w_tier, x_tier))
-                    w_cols = slice(tiles[s] * P, (tiles[s] + 1) * P)
-                    x_cols = slice(first * CH, (first + count) * CH)
+                        sums[block] = sum_pool.tile([P, len(tiles), count * CHUNK], F32, name="sum_bank")
+                    waiting.remove(item)
+                    w_columns = slice(tiles[place] * P, (tiles[place] + 1) * P)
+                    x_columns = slice((first + part) * CHUNK, (first + part) * CHUNK + width)
                     nc.tensor.matmul_mx(
-                        out=sums[n][:, s, :],
-                        lhsT=codes["w", w_tier][:, w_cols].bitcast(FP8X4),
-                        lhsT_scale=scales["w", w_tier][:, w_cols],
-                        rhs=codes["x", x_tier][:, x_cols].bitcast(FP8X4),
-                        rhs_scale=scales["x", x_tier][:, x_cols],
+                        out=sums[block][:, place, part * CHUNK : part * CHUNK + width],
+                        lhsT=codes["w", w_tier][:, w_columns].bitcast(FP8X4),
+                        lhsT_scale=scales["w", w_tier][:, w_columns],
+                        rhs=codes["x", x_tier][:, x_columns].bitcast(FP8X4),
+                        rhs_scale=scales["x", x_tier][:, x_columns],
                         start=opening,
-                        stop=all(item[0] != n for item in waiting),
+                        stop=all(other[0] != block for other in waiting),
                     )
-                    columns = columns - count * CH
+                    budget = budget - width
 
-        def finish(n):
-            first, count, tiles = blocks[n]
-            result = sb.tile([P, len(tiles), count * CH], F32, name="result%d" % n, align_bytes=64)
-            together = min(2, len(tiles))
-            for s, c in enumerate(tiles):
+        def finish(block):
+            first, count, tiles = blocks[block]
+            result = sb.tile([P, len(tiles), count * CHUNK], F32, name="result%d" % block, align_bytes=64)
+            together = min(STORE_TILES, len(tiles))
+            for place, c in enumerate(tiles):
                 nc.scalar.activation(
-                    out=result[:, s, :], in_=sums[n][:, s, :], func=ACT.Gelu_apprx_tanh, bias=bias[:, c : c + 1]
+                    out=result[:, place, :], in_=sums[block][:, place, :], func=GELU, bias=bias[:, c : c + 1]
                 )
-                if (s + 1) % together == 0:
+                if (place + 1) % together == 0:
                     nc.sync.dma_start(
-                        out=out_rows[:, c + 1 - together : c + 1, first * CH : (first + count) * CH],
-                        in_=result[:, s + 1 - together : s + 1, :],
+                        out=out_rows[:, c + 1 - together : c + 1, first * CHUNK : (first + count) * CHUNK],
+                        in_=result[:, place + 1 - together : place + 1, :],
                     )
 
         last = len(order) - 1
-        for s in range(len(order)):
-            cast(order[s], s == 0)
-            if s < 2:
-                quantise(order[s][0], "q", order[s][1], 1)
-                dequantise(order[s])
-        quantised = 2
-        returned = 2
+        primed = 2
+        for s, chunk in enumerate(order):
+            round_and_interleave(chunk, s == 0)
+            if s < primed:
+                quantise(chunk, "q")
+                bring_back(chunk)
+
+        first_tier = primed
+        brought = primed
+        finished = 0
         for s in range(len(order) + 1):
             if s <= last:
-                leftover(order[s])
+                subtract(order[s])
             if s > 0:
-                quantise(order[s - 1][0], "r", order[s - 1][1], 1)
-            while quantised <= min(last, 2 + (QN * s) // QD):
-                quantise(order[quantised][0], "q", order[quantised][1], 1)
-                quantised = quantised + 1
-            closing = s - 1 - half
-            for what in ORD:
-                if what == "c" and closing >= 0:
-                    multiply(K * N, closing, closing)
-                    finish(closing)
-                if what == "d":
-                    while returned <= min(quantised - 1, s + AHEAD):
-                        dequantise(order[returned])
-                        returned = returned + 1
-                if what == "m":
-                    multiply(BUDGET, 0, max(closing - REOPEN, -1) + SUM_BANKS)
+                quantise(order[s - 1], "r")
+            while first_tier <= min(last, primed + (3 * s) // 2):
+                quantise(order[first_tier], "q")
+                first_tier = first_tier + 1
+            newest_block = finished + SUM_BANKS - 1
+            while brought <= min(first_tier - 1, s + BACK_BANKS):
+                bring_back(order[brought])
+                brought = brought + 1
+            while finished < len(blocks) and all(ready(*item) for item in waiting if item[0] == finished):
+                multiply(3 * K, finished, finished)
+                finish(finished)
+                finished = finished + 1
+            multiply(FILL_AFTER_FIRST_BLOCK if finished else FILL_BEFORE_FIRST_BLOCK, 0, newest_block)
         assert not waiting

@@ -19,10 +19,10 @@ CHUNK = 128
 RUN = 4
 BACK_BANKS = 3
 SUM_BANKS = 5
-PASS_CHUNKS = 2
-STORE_TILES = 2
-FILL_BEFORE_FIRST_BLOCK = 1024
-FILL_AFTER_FIRST_BLOCK = 640
+BACK_AHEAD = 2
+BANK_REST = 2
+COLUMNS_PER_SUBTRACT = 1024
+COLUMNS_PER_QUANTISE = 256
 
 
 def rows_view(rows):
@@ -45,9 +45,7 @@ def tile_mix_tierb_three_gelu_kernel(tc, w, x, b, out):
         sum_pool = ctx.enter_context(tc.psum_pool(name="sums", bufs=SUM_BANKS))
         ctx.enter_context(tc.manual_schedule())
 
-        loads = [("w", 0, 1), ("w", 1, 1)]
-        loads = loads + [("x", i, 2) for i in range(0, half, 2)] + [("w", 2, 2)]
-        loads = loads + [("x", i, 2) for i in range(half, x_chunks, 2)]
+        loads = [("x", 0, 2), ("w", 0, 2), ("x", 2, 2), ("w", 2, 2), ("x", 4, 2), ("x", 6, 2)]
         matrix = {"w": w, "x": x}
         raw = {}
         order = []
@@ -77,7 +75,12 @@ def tile_mix_tierb_three_gelu_kernel(tc, w, x, b, out):
             )
         id_codes = sb.tile([P, K], U32, name="id_codes", align_bytes=64)
         id_scales = sb.tile([P, K], U8, name="id_scales", align_bytes=64)
-        nc.vector.quantize_mx(out=id_codes[:].bitcast(FP8X4), scales=id_scales[:], in_=identity[:])
+        for columns in (slice(0, K // 2), slice(K // 2, K)):
+            nc.vector.quantize_mx(
+                out=id_codes[:, columns].bitcast(FP8X4),
+                scales=id_scales[:, columns],
+                in_=identity[:, PACK * columns.start : PACK * columns.stop],
+            )
 
         codes = {}
         scales = {}
@@ -96,13 +99,11 @@ def tile_mix_tierb_three_gelu_kernel(tc, w, x, b, out):
             which, i = chunk
             return rounded[which, tier][:, i * CHUNK * PACK : (i + 1) * CHUNK * PACK]
 
-        def round_and_interleave(chunk, shared):
+        def round_and_interleave(chunk, on_vector):
             words = words_view(rounded_chunk(chunk, "q"))
             rows = rows_view(raw[chunk])
-            if shared:
-                cut = CHUNK // RUN // 2
-                nc.scalar.copy(out=words[:, :cut], in_=rows[:, :cut])
-                nc.vector.tensor_copy(out=words[:, cut:], in_=rows[:, cut:])
+            if on_vector:
+                nc.vector.tensor_copy(out=words, in_=rows)
             else:
                 nc.scalar.copy(out=words, in_=rows)
 
@@ -140,32 +141,41 @@ def tile_mix_tierb_three_gelu_kernel(tc, w, x, b, out):
             )
 
         blocks = [(0, half, (c,)) for c in range(n_tiles)]
-        blocks = blocks + [(i, 1, tuple(range(n_tiles))) for i in range(half, x_chunks)]
+        blocks = blocks + [(half, 2, (0, 1)), (half, 2, (2, 3))]
+        blocks = blocks + [(half + 2, 2, (c,)) for c in range(n_tiles)]
         waiting = [
             (block, place, part, w_tier, x_tier)
             for block, (first, count, tiles) in enumerate(blocks)
             for w_tier, x_tier in (("q", "q"), ("r", "q"), ("q", "r"))
             for place in range(len(tiles))
-            for part in range(0, count, PASS_CHUNKS)
+            for part in range(count)
         ]
         sums = {}
         out_rows = out.rearrange("(c p) t -> p c t", p=P)
 
-        def ready(block, place, part, w_tier, x_tier):
+        def ready(known, block, place, part, w_tier, x_tier):
             first, count, tiles = blocks[block]
-            needed = range(first + part, first + min(part + PASS_CHUNKS, count))
-            return ("w", w_tier, tiles[place]) in quantised and all(("x", x_tier, i) in quantised for i in needed)
+            return ("w", w_tier, tiles[place]) in known and ("x", x_tier, first + part) in known
 
-        def multiply(budget, lowest, highest):
+        def multiply(budget, highest, known):
             for item in list(waiting):
                 block, place, part, w_tier, x_tier = item
-                if budget > 0 and lowest <= block <= highest and ready(*item):
+                if item in waiting and budget > 0 and block <= highest and ready(known, *item):
                     first, count, tiles = blocks[block]
-                    width = min(PASS_CHUNKS, count) * CHUNK
+                    run = [item]
+                    for more in range(part + 1, count):
+                        neighbour = (block, place, more, w_tier, x_tier)
+                        if len(run) == more - part and neighbour in waiting and ready(known, *neighbour):
+                            run.append(neighbour)
+                    run = run[: 2 if len(run) == 3 else len(run)]
+                    width = len(run) * CHUNK
                     opening = block not in sums
-                    if opening:
+                    if opening and block < BACK_BANKS + SUM_BANKS:
                         sums[block] = sum_pool.tile([P, len(tiles), count * CHUNK], F32, name="sum_bank")
-                    waiting.remove(item)
+                    elif opening:
+                        sums[block] = back_pool.tile([P, len(tiles), count * CHUNK], F32, name="back_bank")
+                    for done in run:
+                        waiting.remove(done)
                     w_columns = slice(tiles[place] * P, (tiles[place] + 1) * P)
                     x_columns = slice((first + part) * CHUNK, (first + part) * CHUNK + width)
                     nc.tensor.matmul_mx(
@@ -178,11 +188,12 @@ def tile_mix_tierb_three_gelu_kernel(tc, w, x, b, out):
                         stop=all(other[0] != block for other in waiting),
                     )
                     budget = budget - width
+            return budget
 
         def finish(block):
             first, count, tiles = blocks[block]
             result = sb.tile([P, len(tiles), count * CHUNK], F32, name="result%d" % block, align_bytes=64)
-            together = min(STORE_TILES, len(tiles))
+            together = 1
             for place, c in enumerate(tiles):
                 nc.scalar.activation(
                     out=result[:, place, :], in_=sums[block][:, place, :], func=GELU, bias=bias[:, c : c + 1]
@@ -197,28 +208,42 @@ def tile_mix_tierb_three_gelu_kernel(tc, w, x, b, out):
         primed = 2
         for s, chunk in enumerate(order):
             round_and_interleave(chunk, s == 0)
-            if s < primed:
-                quantise(chunk, "q")
-                bring_back(chunk)
+        for chunk in order[:primed]:
+            quantise(chunk, "q")
+            bring_back(chunk)
 
+        steps = []
         first_tier = primed
-        brought = primed
-        finished = 0
         for s in range(len(order) + 1):
-            if s <= last:
-                subtract(order[s])
-            if s > 0:
-                quantise(order[s - 1], "r")
-            while first_tier <= min(last, primed + (3 * s) // 2):
-                quantise(order[first_tier], "q")
-                first_tier = first_tier + 1
-            newest_block = finished + SUM_BANKS - 1
-            while brought <= min(first_tier - 1, s + BACK_BANKS):
+            newest = min(last, primed + (4 * s) // 3)
+            ahead = [("q", m) for m in range(first_tier, newest + 1)]
+            first_tier = newest + 1
+            steps = steps + [("subtract", s)] * (s <= last) + ahead[:1] + [("r", s - 1)] * (s > 0) + ahead[1:]
+        steps = steps + [("none", 0)] * 8
+
+        brought = primed
+        subtracted = 0
+        finished = [0] * BANK_REST
+        credit = 0
+        for kind, m in steps:
+            known = set(quantised)
+            if kind == "subtract":
+                subtract(order[m])
+                subtracted = m + 1
+            elif kind != "none":
+                quantise(order[m], kind)
+            credit = min(credit, 0) + (COLUMNS_PER_QUANTISE if kind in ("q", "r") else COLUMNS_PER_SUBTRACT)
+            while brought <= min(last, subtracted - 1 + BACK_AHEAD) and (order[brought][0], "q", order[brought][1]) in known:
                 bring_back(order[brought])
                 brought = brought + 1
-            while finished < len(blocks) and all(ready(*item) for item in waiting if item[0] == finished):
-                multiply(3 * K, finished, finished)
-                finish(finished)
-                finished = finished + 1
-            multiply(FILL_AFTER_FIRST_BLOCK if finished else FILL_BEFORE_FIRST_BLOCK, 0, newest_block)
+                credit = credit - PACK * CHUNK
+            highest = finished[-BANK_REST] + SUM_BANKS - 1
+            if highest >= BACK_BANKS + SUM_BANKS - 1:
+                highest = BACK_BANKS + SUM_BANKS - 1 + max(0, subtracted - 1 - (last - BACK_BANKS))
+            credit = multiply(credit, highest, known)
+            done = finished[-1]
+            while done < len(blocks) and all(item[0] != done for item in waiting):
+                finish(done)
+                done = done + 1
+            finished.append(done)
         assert not waiting

@@ -8,19 +8,23 @@ FLOPS = 3 * 2 * K * N * T
 F32 = mybir.dt.float32
 BF16 = mybir.dt.bfloat16
 U32 = mybir.dt.uint32
+I32 = mybir.dt.int32
 U8 = mybir.dt.uint8
 FP8X4 = mybir.dt.float8_e4m3fn_x4
 ALU = mybir.AluOpType
 GELU = mybir.ActivationFunctionType.Gelu_apprx_tanh
 
 P = 128
+BF16_ONE = 0x3F80
 PACK = 4
 CHUNK = 128
 RUN = 4
 BACK_BANKS = 3
 SUM_BANKS = 5
 BACK_AHEAD = 2
-BANK_REST = 2
+SPLIT_FROM = 99
+SCALAR_GROUPS = 10
+BANK_REST = 1
 COLUMNS_PER_SUBTRACT = 1024
 COLUMNS_PER_QUANTISE = 256
 
@@ -45,7 +49,7 @@ def tile_mix_tierb_three_gelu_kernel(tc, w, x, b, out):
         sum_pool = ctx.enter_context(tc.psum_pool(name="sums", bufs=SUM_BANKS))
         ctx.enter_context(tc.manual_schedule())
 
-        loads = [("x", 0, 2), ("w", 0, 2), ("x", 2, 2), ("w", 2, 2), ("x", 4, 2), ("x", 6, 2)]
+        loads = [("w", 0, 1), ("x", 0, 1), ("w", 1, 1), ("x", 1, 1), ("x", 2, 2), ("w", 2, 2), ("x", 4, 2), ("x", 6, 2)]
         matrix = {"w": w, "x": x}
         raw = {}
         order = []
@@ -64,14 +68,19 @@ def tile_mix_tierb_three_gelu_kernel(tc, w, x, b, out):
         nc.vector.memset(table_warm[:, 0:1], 0.0)
         nc.scalar.activation(out=table_warm[:, 1:2], in_=table_warm[:, 0:1], func=GELU)
 
-        ramp = sb.tile([P, K], BF16, name="ramp", align_bytes=64)
+        ramp = sb.tile([P, K // 2], BF16, name="ramp", align_bytes=64)
         nc.gpsimd.iota(
-            ramp[:], pattern=[[1, K]], base=0, channel_multiplier=-PACK, allow_small_or_imprecise_dtypes=True
+            ramp[:], pattern=[[1, K // 2]], base=0, channel_multiplier=-2, allow_small_or_imprecise_dtypes=True
         )
         identity = sb.tile([P, PACK * K], BF16, name="identity", align_bytes=64)
         for j in range(PACK):
             nc.vector.tensor_scalar(
-                out=identity[:, j * K : (j + 1) * K], in0=ramp[:], scalar1=float(j), scalar2=None, op0=ALU.is_equal
+                out=identity[:, j * K : (j + 1) * K].bitcast(I32),
+                in0=ramp[:],
+                scalar1=float(j // 2),
+                scalar2=float(BF16_ONE << (16 * (j % 2))),
+                op0=ALU.is_equal,
+                op1=ALU.mult,
             )
         id_codes = sb.tile([P, K], U32, name="id_codes", align_bytes=64)
         id_scales = sb.tile([P, K], U8, name="id_scales", align_bytes=64)
@@ -99,9 +108,9 @@ def tile_mix_tierb_three_gelu_kernel(tc, w, x, b, out):
             which, i = chunk
             return rounded[which, tier][:, i * CHUNK * PACK : (i + 1) * CHUNK * PACK]
 
-        def round_and_interleave(chunk, on_vector):
-            words = words_view(rounded_chunk(chunk, "q"))
-            rows = rows_view(raw[chunk])
+        def round_and_interleave(chunk, groups, on_vector):
+            words = words_view(rounded_chunk(chunk, "q"))[:, groups]
+            rows = rows_view(raw[chunk])[:, groups]
             if on_vector:
                 nc.vector.tensor_copy(out=words, in_=rows)
             else:
@@ -132,17 +141,15 @@ def tile_mix_tierb_three_gelu_kernel(tc, w, x, b, out):
                     stop=True,
                 )
 
-        def subtract(chunk):
+        def subtract(chunk, groups):
             nc.vector.tensor_tensor(
-                out=words_view(rounded_chunk(chunk, "r")),
-                in0=rows_view(raw[chunk]),
-                in1=rows_view(back[chunk][:]),
+                out=words_view(rounded_chunk(chunk, "r"))[:, groups],
+                in0=rows_view(raw[chunk])[:, groups],
+                in1=rows_view(back[chunk][:])[:, groups],
                 op=ALU.subtract,
             )
 
-        blocks = [(0, half, (c,)) for c in range(n_tiles)]
-        blocks = blocks + [(half, 2, (0, 1)), (half, 2, (2, 3))]
-        blocks = blocks + [(half + 2, 2, (c,)) for c in range(n_tiles)]
+        blocks = [(0, 4, (0,)),(0, 4, (1,)),(0, 4, (2,)),(0, 4, (3,)),(4, 1, (0, 1, 2, 3)),(5, 1, (0, 1, 2, 3)),(6, 2, (0,)),(6, 2, (1,)),(6, 2, (2,)),(6, 2, (3,))]
         waiting = [
             (block, place, part, w_tier, x_tier)
             for block, (first, count, tiles) in enumerate(blocks)
@@ -193,7 +200,7 @@ def tile_mix_tierb_three_gelu_kernel(tc, w, x, b, out):
         def finish(block):
             first, count, tiles = blocks[block]
             result = sb.tile([P, len(tiles), count * CHUNK], F32, name="result%d" % block, align_bytes=64)
-            together = 1
+            together = min(2, len(tiles))
             for place, c in enumerate(tiles):
                 nc.scalar.activation(
                     out=result[:, place, :], in_=sums[block][:, place, :], func=GELU, bias=bias[:, c : c + 1]
@@ -205,34 +212,44 @@ def tile_mix_tierb_three_gelu_kernel(tc, w, x, b, out):
                     )
 
         last = len(order) - 1
-        primed = 2
+        on_vector = (0, 1)
         for s, chunk in enumerate(order):
-            round_and_interleave(chunk, s == 0)
-        for chunk in order[:primed]:
-            quantise(chunk, "q")
-            bring_back(chunk)
+            round_and_interleave(chunk, slice(0, SCALAR_GROUPS if s in on_vector else CHUNK // RUN), False)
 
-        steps = []
-        first_tier = primed
+        steps = [("round", 0), ("q", 0), ("round", 1), ("q", 1)]
+        first_tier = 2
         for s in range(len(order) + 1):
-            newest = min(last, primed + (4 * s) // 3)
+            newest = min(last, 2 + (4 * s) // 3)
             ahead = [("q", m) for m in range(first_tier, newest + 1)]
-            first_tier = newest + 1
-            steps = steps + [("subtract", s)] * (s <= last) + ahead[:1] + [("r", s - 1)] * (s > 0) + ahead[1:]
+            first_tier = max(first_tier, newest + 1)
+            if s > last:
+                steps = steps + [("r", last)]
+            elif s >= SPLIT_FROM:
+                steps = steps + [("left", s), ("r", s - 1), ("right", s)]
+            else:
+                steps = steps + [("subtract", s)] + ahead[:1] + [("r", s - 1)] * (s > 0) + ahead[1:]
         steps = steps + [("none", 0)] * 8
 
-        brought = primed
+        brought = 0
         subtracted = 0
         finished = [0] * BANK_REST
         credit = 0
         for kind, m in steps:
             known = set(quantised)
-            if kind == "subtract":
-                subtract(order[m])
+            if kind == "round":
+                round_and_interleave(order[m], slice(SCALAR_GROUPS, CHUNK // RUN), True)
+            elif kind == "subtract":
+                subtract(order[m], slice(0, CHUNK // RUN))
+                subtracted = m + 1
+            elif kind == "left":
+                subtract(order[m], slice(0, CHUNK // RUN // 2))
+            elif kind == "right":
+                subtract(order[m], slice(CHUNK // RUN // 2, CHUNK // RUN))
                 subtracted = m + 1
             elif kind != "none":
                 quantise(order[m], kind)
-            credit = min(credit, 0) + (COLUMNS_PER_QUANTISE if kind in ("q", "r") else COLUMNS_PER_SUBTRACT)
+            share = {"subtract": 1.0, "none": 1.0, "left": 0.5, "right": 0.5}
+            credit = min(credit, 0) + (share[kind] * COLUMNS_PER_SUBTRACT if kind in share else COLUMNS_PER_QUANTISE)
             while brought <= min(last, subtracted - 1 + BACK_AHEAD) and (order[brought][0], "q", order[brought][1]) in known:
                 bring_back(order[brought])
                 brought = brought + 1

@@ -22,11 +22,21 @@ RUN = 4
 BACK_BANKS = 3
 SUM_BANKS = 5
 BACK_AHEAD = 2
-SPLIT_FROM = 99
-SCALAR_GROUPS = 10
-BANK_REST = 1
-COLUMNS_PER_SUBTRACT = 1024
-COLUMNS_PER_QUANTISE = 256
+STEPS = "R0 q0 R1 q1 s0 q2 s1 q3 r0 r1 s2 q4 q5 r2 s3 q6 s4 q7 r3 r4 s5 q8 s6 q9 r5 r6 s7 qa s8 qb r7 r8 s9 sa r9 sb ra rb"
+SPARE = 2
+ORDER = "w0 x0 w1 x1 x2 x3 w2 w3 x4 x5 x6 x7"
+LOADS = (1, 1, 1, 1, 1, 1, 1, 1, 2, 2)
+SHARED = (10, 10)
+BLOCKS = ((0, 2, (0, 1)), (2, 2, (0, 1)), (0, 4, (2,)), (0, 4, (3,)), (4, 1, (0, 1, 2, 3)), (5, 1, (0, 1, 2, 3)), (6, 2, (0,)), (6, 2, (1,)), (6, 2, (2,)), (6, 2, (3,)))
+PER_SUB = 1024
+PER_Q = 256
+WARM = 4
+GELU_AFTER = 99
+MINW = 6
+TOGETHER = 2
+TAIL_BLOCKS = 99
+BIAS_AT = 99
+HEAD = 2
 
 
 def rows_view(rows):
@@ -49,20 +59,23 @@ def tile_mix_tierb_three_gelu_kernel(tc, w, x, b, out):
         sum_pool = ctx.enter_context(tc.psum_pool(name="sums", bufs=SUM_BANKS))
         ctx.enter_context(tc.manual_schedule())
 
-        loads = [("w", 0, 1), ("x", 0, 1), ("w", 1, 1), ("x", 1, 1), ("x", 2, 2), ("w", 2, 2), ("x", 4, 2), ("x", 6, 2)]
+        order = [(name[0], int(name[1])) for name in ORDER.split()]
         matrix = {"w": w, "x": x}
         raw = {}
-        order = []
-        for which, first, count in loads:
+        bias = sb.tile([P, n_tiles], F32, name="bias", align_bytes=64)
+        at = 0
+        for number, count in enumerate(LOADS):
+            which, first = order[at]
+            assert order[at + count - 1] == (which, first + count - 1)
             landed = sb.tile([P, PACK, count * CHUNK], F32, name="raw_%s%d" % (which, first), align_bytes=64)
             columns = matrix[which][:, first * CHUNK : (first + count) * CHUNK]
             nc.sync.dma_start(out=landed[:], in_=columns.rearrange("(p j) c -> p j c", j=PACK))
             for i in range(count):
                 raw[which, first + i] = landed[:, :, i * CHUNK : (i + 1) * CHUNK]
-                order.append((which, first + i))
-        bias = sb.tile([P, n_tiles], F32, name="bias", align_bytes=64)
-        with nc.allow_non_contiguous_dma(reason="one bias value for each partition and n tile"):
-            nc.sync.dma_start(out=bias[:], in_=b.rearrange("(c p) -> p c", p=P))
+            at = at + count
+            if number + 1 == min(BIAS_AT, len(LOADS)):
+                with nc.allow_non_contiguous_dma(reason="one bias value for each partition and n tile"):
+                    nc.sync.dma_start(out=bias[:], in_=b.rearrange("(c p) -> p c", p=P))
 
         table_warm = sb.tile([P, 2], F32, name="table_warm", align_bytes=64)
         nc.vector.memset(table_warm[:, 0:1], 0.0)
@@ -73,7 +86,10 @@ def tile_mix_tierb_three_gelu_kernel(tc, w, x, b, out):
             ramp[:], pattern=[[1, K // 2]], base=0, channel_multiplier=-2, allow_small_or_imprecise_dtypes=True
         )
         identity = sb.tile([P, PACK * K], BF16, name="identity", align_bytes=64)
-        for j in range(PACK):
+        id_codes = sb.tile([P, K], U32, name="id_codes", align_bytes=64)
+        id_scales = sb.tile([P, K], U8, name="id_scales", align_bytes=64)
+
+        def write_identity(j):
             nc.vector.tensor_scalar(
                 out=identity[:, j * K : (j + 1) * K].bitcast(I32),
                 in0=ramp[:],
@@ -82,31 +98,47 @@ def tile_mix_tierb_three_gelu_kernel(tc, w, x, b, out):
                 op0=ALU.is_equal,
                 op1=ALU.mult,
             )
-        id_codes = sb.tile([P, K], U32, name="id_codes", align_bytes=64)
-        id_scales = sb.tile([P, K], U8, name="id_scales", align_bytes=64)
-        for columns in (slice(0, K // 2), slice(K // 2, K)):
+
+        def quantise_identity(columns):
             nc.vector.quantize_mx(
                 out=id_codes[:, columns].bitcast(FP8X4),
                 scales=id_scales[:, columns],
                 in_=identity[:, PACK * columns.start : PACK * columns.stop],
             )
 
+        first_half = slice(0, K // 2)
+        write_identity(0)
+        write_identity(1)
+        write_identity(2)
+        quantise_identity(first_half)
+        write_identity(3)
+        warm_bank = sum_pool.tile([P, K // 2], F32, name="sum_bank")
+        for i in range(WARM):
+            nc.tensor.matmul_mx(
+                out=warm_bank[:],
+                lhsT=id_codes[:, 0:P].bitcast(FP8X4),
+                lhsT_scale=id_scales[:, 0:P],
+                rhs=id_codes[:, first_half].bitcast(FP8X4),
+                rhs_scale=id_scales[:, first_half],
+                start=True,
+                stop=True,
+            )
+        quantise_identity(slice(K // 2, K))
+
         codes = {}
         scales = {}
+        rounded = {}
         for which, width in (("w", N), ("x", T)):
             for tier in ("q", "r"):
                 codes[which, tier] = sb.tile([P, width], U32, name="codes_" + which + tier, align_bytes=64)
                 scales[which, tier] = sb.tile([P, width], U8, name="scales_" + which + tier, align_bytes=64)
-        rounded = {}
-        for which, width in (("w", N), ("x", T)):
-            for tier in ("q", "r"):
                 rounded[which, tier] = sb.tile([P, PACK * width], BF16, name="bf_" + which + tier, align_bytes=64)
         quantised = set()
         back = {}
 
-        def rounded_chunk(chunk, tier):
+        def rounded_chunk(chunk, tier, count=1):
             which, i = chunk
-            return rounded[which, tier][:, i * CHUNK * PACK : (i + 1) * CHUNK * PACK]
+            return rounded[which, tier][:, i * CHUNK * PACK : (i + count) * CHUNK * PACK]
 
         def round_and_interleave(chunk, groups, on_vector):
             words = words_view(rounded_chunk(chunk, "q"))[:, groups]
@@ -116,15 +148,18 @@ def tile_mix_tierb_three_gelu_kernel(tc, w, x, b, out):
             else:
                 nc.scalar.copy(out=words, in_=rows)
 
-        def quantise(chunk, tier):
-            which, i = chunk
-            columns = slice(i * CHUNK, (i + 1) * CHUNK)
+        def quantise(places, tier):
+            which, i = order[places[0]]
+            count = len(places)
+            assert order[places[-1]] == (which, i + count - 1)
+            columns = slice(i * CHUNK, (i + count) * CHUNK)
             nc.vector.quantize_mx(
                 out=codes[which, tier][:, columns].bitcast(FP8X4),
                 scales=scales[which, tier][:, columns],
-                in_=rounded_chunk(chunk, tier),
+                in_=rounded_chunk((which, i), tier, count),
             )
-            quantised.add((which, tier, i))
+            for more in range(count):
+                quantised.add((which, tier, i + more))
 
         def bring_back(chunk):
             which, i = chunk
@@ -149,7 +184,7 @@ def tile_mix_tierb_three_gelu_kernel(tc, w, x, b, out):
                 op=ALU.subtract,
             )
 
-        blocks = [(0, 4, (0,)),(0, 4, (1,)),(0, 4, (2,)),(0, 4, (3,)),(4, 1, (0, 1, 2, 3)),(5, 1, (0, 1, 2, 3)),(6, 2, (0,)),(6, 2, (1,)),(6, 2, (2,)),(6, 2, (3,))]
+        blocks = list(BLOCKS)
         waiting = [
             (block, place, part, w_tier, x_tier)
             for block, (first, count, tiles) in enumerate(blocks)
@@ -164,7 +199,7 @@ def tile_mix_tierb_three_gelu_kernel(tc, w, x, b, out):
             first, count, tiles = blocks[block]
             return ("w", w_tier, tiles[place]) in known and ("x", x_tier, first + part) in known
 
-        def multiply(budget, highest, known):
+        def multiply(budget, highest, known, narrowest, spare):
             for item in list(waiting):
                 block, place, part, w_tier, x_tier = item
                 if item in waiting and budget > 0 and block <= highest and ready(known, *item):
@@ -175,9 +210,11 @@ def tile_mix_tierb_three_gelu_kernel(tc, w, x, b, out):
                         if len(run) == more - part and neighbour in waiting and ready(known, *neighbour):
                             run.append(neighbour)
                     run = run[: 2 if len(run) == 3 else len(run)]
+                    if len(run) < min(narrowest, count) and part % 2 == 0:
+                        continue
                     width = len(run) * CHUNK
                     opening = block not in sums
-                    if opening and block < BACK_BANKS + SUM_BANKS:
+                    if opening and block < len(blocks) - spare:
                         sums[block] = sum_pool.tile([P, len(tiles), count * CHUNK], F32, name="sum_bank")
                     elif opening:
                         sums[block] = back_pool.tile([P, len(tiles), count * CHUNK], F32, name="back_bank")
@@ -200,7 +237,7 @@ def tile_mix_tierb_three_gelu_kernel(tc, w, x, b, out):
         def finish(block):
             first, count, tiles = blocks[block]
             result = sb.tile([P, len(tiles), count * CHUNK], F32, name="result%d" % block, align_bytes=64)
-            together = min(2, len(tiles))
+            together = min(TOGETHER if block >= len(blocks) - TAIL_BLOCKS else 4, len(tiles))
             for place, c in enumerate(tiles):
                 nc.scalar.activation(
                     out=result[:, place, :], in_=sums[block][:, place, :], func=GELU, bias=bias[:, c : c + 1]
@@ -212,52 +249,52 @@ def tile_mix_tierb_three_gelu_kernel(tc, w, x, b, out):
                     )
 
         last = len(order) - 1
-        on_vector = (0, 1)
-        for s, chunk in enumerate(order):
-            round_and_interleave(chunk, slice(0, SCALAR_GROUPS if s in on_vector else CHUNK // RUN), False)
+        groups = CHUNK // RUN
+        shared = list(SHARED) + [groups] * len(order)
+        early = min(GELU_AFTER, len(order))
+        for s in range(early):
+            if shared[s]:
+                round_and_interleave(order[s], slice(0, shared[s]), False)
+        late_rounds = list(range(early, len(order)))
 
-        steps = [("round", 0), ("q", 0), ("round", 1), ("q", 1)]
-        first_tier = 2
-        for s in range(len(order) + 1):
-            newest = min(last, 2 + (4 * s) // 3)
-            ahead = [("q", m) for m in range(first_tier, newest + 1)]
-            first_tier = max(first_tier, newest + 1)
-            if s > last:
-                steps = steps + [("r", last)]
-            elif s >= SPLIT_FROM:
-                steps = steps + [("left", s), ("r", s - 1), ("right", s)]
-            else:
-                steps = steps + [("subtract", s)] + ahead[:1] + [("r", s - 1)] * (s > 0) + ahead[1:]
-        steps = steps + [("none", 0)] * 8
+        steps = []
+        for word in STEPS.split():
+            steps.append((word[0], tuple(int(c, 16) for c in word[1:])))
+        steps = steps + [("n", (0,))] * 8
+        half = groups // 2
 
         brought = 0
         subtracted = 0
-        finished = [0] * BANK_REST
+        finished = [0]
         credit = 0
-        for kind, m in steps:
+        for kind, places in steps:
             known = set(quantised)
-            if kind == "round":
-                round_and_interleave(order[m], slice(SCALAR_GROUPS, CHUNK // RUN), True)
-            elif kind == "subtract":
-                subtract(order[m], slice(0, CHUNK // RUN))
-                subtracted = m + 1
-            elif kind == "left":
-                subtract(order[m], slice(0, CHUNK // RUN // 2))
-            elif kind == "right":
-                subtract(order[m], slice(CHUNK // RUN // 2, CHUNK // RUN))
-                subtracted = m + 1
-            elif kind != "none":
-                quantise(order[m], kind)
-            share = {"subtract": 1.0, "none": 1.0, "left": 0.5, "right": 0.5}
-            credit = min(credit, 0) + (share[kind] * COLUMNS_PER_SUBTRACT if kind in share else COLUMNS_PER_QUANTISE)
+            if kind == "R":
+                round_and_interleave(order[places[0]], slice(shared[places[0]], groups), True)
+            elif kind == "S":
+                round_and_interleave(order[places[0]], slice(0, groups), False)
+                continue
+            elif kind == "s":
+                subtract(order[places[0]], slice(0, groups))
+                subtracted = places[0] + 1
+            elif kind == "a":
+                subtract(order[places[0]], slice(0, half))
+            elif kind == "b":
+                subtract(order[places[0]], slice(half, groups))
+                subtracted = places[0] + 1
+            elif kind != "n":
+                quantise(places, kind)
+            credit = min(credit, 0) + (PER_SUB if kind in "sn" else PER_SUB // 2 if kind in "ab" else PER_Q * len(places))
             while brought <= min(last, subtracted - 1 + BACK_AHEAD) and (order[brought][0], "q", order[brought][1]) in known:
                 bring_back(order[brought])
                 brought = brought + 1
                 credit = credit - PACK * CHUNK
-            highest = finished[-BANK_REST] + SUM_BANKS - 1
-            if highest >= BACK_BANKS + SUM_BANKS - 1:
-                highest = BACK_BANKS + SUM_BANKS - 1 + max(0, subtracted - 1 - (last - BACK_BANKS))
-            credit = multiply(credit, highest, known)
+            spare = SPARE
+            highest = finished[-1] + SUM_BANKS - 1
+            limit = len(blocks) - spare - 1
+            if highest >= limit:
+                highest = limit + max(0, min(spare, subtracted - (last + 1 - BACK_BANKS)))
+            credit = multiply(credit, highest, known, 2 if subtracted >= MINW else 1, spare)
             done = finished[-1]
             while done < len(blocks) and all(item[0] != done for item in waiting):
                 finish(done)

@@ -19,24 +19,20 @@ BF16_ONE = 0x3F80
 PACK = 4
 CHUNK = 128
 RUN = 4
+GROUPS = CHUNK // RUN
+
+SINGLE_LOADS = 8
+SHARED_CHUNKS = 2
+SCALAR_GROUPS = 10
+FIRST_TIER_AHEAD = 3
 BACK_BANKS = 3
 SUM_BANKS = 5
-BACK_AHEAD = 2
-STEPS = "R0 q0 R1 q1 s0 q2 s1 q3 r0 r1 s2 q4 q5 r2 s3 q6 s4 q7 r3 r4 s5 q8 s6 q9 r5 r6 s7 qa s8 qb r7 r8 s9 sa r9 sb ra rb"
-SPARE = 2
-ORDER = "w0 x0 w1 x1 x2 x3 w2 w3 x4 x5 x6 x7"
-LOADS = (1, 1, 1, 1, 1, 1, 1, 1, 2, 2)
-SHARED = (10, 10)
-BLOCKS = ((0, 2, (0, 1)), (2, 2, (0, 1)), (0, 4, (2,)), (0, 4, (3,)), (4, 1, (0, 1, 2, 3)), (5, 1, (0, 1, 2, 3)), (6, 2, (0,)), (6, 2, (1,)), (6, 2, (2,)), (6, 2, (3,)))
-PER_SUB = 1024
-PER_Q = 256
-WARM = 4
-GELU_AFTER = 99
-MINW = 6
-TOGETHER = 2
-TAIL_BLOCKS = 99
-BIAS_AT = 99
-HEAD = 2
+BACK_AHEAD = BACK_BANKS - 1
+COLUMNS_PER_SUBTRACT = 1024
+COLUMNS_PER_OTHER = 256
+WIDE_FROM = 6
+STORE_TILES = 2
+TENSOR_WARM_UPS = 5
 
 
 def rows_view(rows):
@@ -47,11 +43,40 @@ def words_view(interleaved):
     return interleaved.rearrange("p (g i j) -> p g j i", i=RUN, j=PACK)
 
 
+def chunk_columns(index, count=1):
+    return slice(index * CHUNK, (index + count) * CHUNK)
+
+
 def tile_mix_tierb_three_gelu_kernel(tc, w, x, b, out):
     nc = tc.nc
     n_tiles = N // P
-    x_chunks = T // CHUNK
-    half = x_chunks // 2
+    quarter = T // CHUNK // 4
+
+    order = [(which, i) for i in range(quarter) for which in ("w", "x")]
+    order = order + [("x", i) for i in range(quarter, 2 * quarter)]
+    order = order + [("w", i) for i in range(quarter, n_tiles)]
+    order = order + [("x", i) for i in range(2 * quarter, 4 * quarter)]
+    last = len(order) - 1
+
+    panels = [(q * quarter, quarter, tuple(range(quarter))) for q in range(2)]
+    panels = panels + [(0, 2 * quarter, (c,)) for c in range(quarter, n_tiles)]
+    panels = panels + [(i, 1, tuple(range(n_tiles))) for i in range(2 * quarter, 3 * quarter)]
+    panels = panels + [(3 * quarter, quarter, (c,)) for c in range(n_tiles)]
+    late_panels = len(panels) - BACK_BANKS - SUM_BANKS
+
+    steps = [(kind, m) for m in range(SHARED_CHUNKS) for kind in ("round", "q")]
+    first_tier = SHARED_CHUNKS
+    leftover = 0
+    for s in range(len(order)):
+        lead = SHARED_CHUNKS if s < SHARED_CHUNKS else FIRST_TIER_AHEAD
+        newest = min(last, s + lead)
+        between = [("q", m) for m in range(first_tier, newest + 1)] + [("r", m) for m in range(leftover, s)]
+        first_tier = newest + 1
+        leftover = s
+        if len(between) >= 2 or s == last:
+            between.append(("r", s))
+            leftover = s + 1
+        steps = steps + [("subtract", s)] + between
 
     with ExitStack() as ctx:
         sb = ctx.enter_context(tc.tile_pool(name="sb", bufs=1))
@@ -59,23 +84,19 @@ def tile_mix_tierb_three_gelu_kernel(tc, w, x, b, out):
         sum_pool = ctx.enter_context(tc.psum_pool(name="sums", bufs=SUM_BANKS))
         ctx.enter_context(tc.manual_schedule())
 
-        order = [(name[0], int(name[1])) for name in ORDER.split()]
         matrix = {"w": w, "x": x}
         raw = {}
         bias = sb.tile([P, n_tiles], F32, name="bias", align_bytes=64)
-        at = 0
-        for number, count in enumerate(LOADS):
-            which, first = order[at]
-            assert order[at + count - 1] == (which, first + count - 1)
+        for place in list(range(SINGLE_LOADS)) + list(range(SINGLE_LOADS, len(order), 2)):
+            which, first = order[place]
+            count = 1 if place < SINGLE_LOADS else 2
             landed = sb.tile([P, PACK, count * CHUNK], F32, name="raw_%s%d" % (which, first), align_bytes=64)
-            columns = matrix[which][:, first * CHUNK : (first + count) * CHUNK]
-            nc.sync.dma_start(out=landed[:], in_=columns.rearrange("(p j) c -> p j c", j=PACK))
+            rows = matrix[which][:, chunk_columns(first, count)].rearrange("(p j) c -> p j c", j=PACK)
+            nc.sync.dma_start(out=landed[:], in_=rows)
             for i in range(count):
-                raw[which, first + i] = landed[:, :, i * CHUNK : (i + 1) * CHUNK]
-            at = at + count
-            if number + 1 == min(BIAS_AT, len(LOADS)):
-                with nc.allow_non_contiguous_dma(reason="one bias value for each partition and n tile"):
-                    nc.sync.dma_start(out=bias[:], in_=b.rearrange("(c p) -> p c", p=P))
+                raw[which, first + i] = landed[:, :, chunk_columns(i)]
+        with nc.allow_non_contiguous_dma(reason="one bias value for each partition and n tile"):
+            nc.sync.dma_start(out=bias[:], in_=b.rearrange("(c p) -> p c", p=P))
 
         table_warm = sb.tile([P, 2], F32, name="table_warm", align_bytes=64)
         nc.vector.memset(table_warm[:, 0:1], 0.0)
@@ -88,6 +109,8 @@ def tile_mix_tierb_three_gelu_kernel(tc, w, x, b, out):
         identity = sb.tile([P, PACK * K], BF16, name="identity", align_bytes=64)
         id_codes = sb.tile([P, K], U32, name="id_codes", align_bytes=64)
         id_scales = sb.tile([P, K], U8, name="id_scales", align_bytes=64)
+        low_half = slice(0, K // 2)
+        high_half = slice(K // 2, K)
 
         def write_identity(j):
             nc.vector.tensor_scalar(
@@ -106,24 +129,23 @@ def tile_mix_tierb_three_gelu_kernel(tc, w, x, b, out):
                 in_=identity[:, PACK * columns.start : PACK * columns.stop],
             )
 
-        first_half = slice(0, K // 2)
-        write_identity(0)
-        write_identity(1)
-        write_identity(2)
-        quantise_identity(first_half)
-        write_identity(3)
+        for j in range(PACK - 1):
+            write_identity(j)
+        quantise_identity(low_half)
+        write_identity(PACK - 1)
+
         warm_bank = sum_pool.tile([P, K // 2], F32, name="sum_bank")
-        for i in range(WARM):
+        for repeat in range(TENSOR_WARM_UPS):
             nc.tensor.matmul_mx(
                 out=warm_bank[:],
                 lhsT=id_codes[:, 0:P].bitcast(FP8X4),
                 lhsT_scale=id_scales[:, 0:P],
-                rhs=id_codes[:, first_half].bitcast(FP8X4),
-                rhs_scale=id_scales[:, first_half],
+                rhs=id_codes[:, low_half].bitcast(FP8X4),
+                rhs_scale=id_scales[:, low_half],
                 start=True,
                 stop=True,
             )
-        quantise_identity(slice(K // 2, K))
+        quantise_identity(high_half)
 
         codes = {}
         scales = {}
@@ -136,58 +158,44 @@ def tile_mix_tierb_three_gelu_kernel(tc, w, x, b, out):
         quantised = set()
         back = {}
 
-        def rounded_chunk(chunk, tier, count=1):
+        def rounded_chunk(chunk, tier):
             which, i = chunk
-            return rounded[which, tier][:, i * CHUNK * PACK : (i + count) * CHUNK * PACK]
+            return rounded[which, tier][:, i * CHUNK * PACK : (i + 1) * CHUNK * PACK]
 
-        def round_and_interleave(chunk, groups, on_vector):
-            words = words_view(rounded_chunk(chunk, "q"))[:, groups]
-            rows = rows_view(raw[chunk])[:, groups]
-            if on_vector:
-                nc.vector.tensor_copy(out=words, in_=rows)
-            else:
-                nc.scalar.copy(out=words, in_=rows)
-
-        def quantise(places, tier):
-            which, i = order[places[0]]
-            count = len(places)
-            assert order[places[-1]] == (which, i + count - 1)
-            columns = slice(i * CHUNK, (i + count) * CHUNK)
+        def quantise(chunk, tier):
+            which, i = chunk
             nc.vector.quantize_mx(
-                out=codes[which, tier][:, columns].bitcast(FP8X4),
-                scales=scales[which, tier][:, columns],
-                in_=rounded_chunk((which, i), tier, count),
+                out=codes[which, tier][:, chunk_columns(i)].bitcast(FP8X4),
+                scales=scales[which, tier][:, chunk_columns(i)],
+                in_=rounded_chunk(chunk, tier),
             )
-            for more in range(count):
-                quantised.add((which, tier, i + more))
+            quantised.add((which, tier, i))
 
         def bring_back(chunk):
             which, i = chunk
-            columns = slice(i * CHUNK, (i + 1) * CHUNK)
             back[chunk] = back_pool.tile([P, PACK, CHUNK], F32, name="back_bank")
             for j in range(PACK):
                 nc.tensor.matmul_mx(
                     out=back[chunk][:, j, :],
                     lhsT=id_codes[:, j * P : (j + 1) * P].bitcast(FP8X4),
                     lhsT_scale=id_scales[:, j * P : (j + 1) * P],
-                    rhs=codes[which, "q"][:, columns].bitcast(FP8X4),
-                    rhs_scale=scales[which, "q"][:, columns],
+                    rhs=codes[which, "q"][:, chunk_columns(i)].bitcast(FP8X4),
+                    rhs_scale=scales[which, "q"][:, chunk_columns(i)],
                     start=True,
                     stop=True,
                 )
 
-        def subtract(chunk, groups):
+        def subtract(chunk):
             nc.vector.tensor_tensor(
-                out=words_view(rounded_chunk(chunk, "r"))[:, groups],
-                in0=rows_view(raw[chunk])[:, groups],
-                in1=rows_view(back[chunk][:])[:, groups],
+                out=words_view(rounded_chunk(chunk, "r")),
+                in0=rows_view(raw[chunk]),
+                in1=rows_view(back[chunk][:]),
                 op=ALU.subtract,
             )
 
-        blocks = list(BLOCKS)
         waiting = [
-            (block, place, part, w_tier, x_tier)
-            for block, (first, count, tiles) in enumerate(blocks)
+            (panel, place, part, w_tier, x_tier)
+            for panel, (first, count, tiles) in enumerate(panels)
             for w_tier, x_tier in (("q", "q"), ("r", "q"), ("q", "r"))
             for place in range(len(tiles))
             for part in range(count)
@@ -195,109 +203,97 @@ def tile_mix_tierb_three_gelu_kernel(tc, w, x, b, out):
         sums = {}
         out_rows = out.rearrange("(c p) t -> p c t", p=P)
 
-        def ready(known, block, place, part, w_tier, x_tier):
-            first, count, tiles = blocks[block]
+        def ready(known, panel, place, part, w_tier, x_tier):
+            first, count, tiles = panels[panel]
             return ("w", w_tier, tiles[place]) in known and ("x", x_tier, first + part) in known
 
-        def multiply(budget, highest, known, narrowest, spare):
+        def multiply(budget, highest, known, wide):
             for item in list(waiting):
-                block, place, part, w_tier, x_tier = item
-                if item in waiting and budget > 0 and block <= highest and ready(known, *item):
-                    first, count, tiles = blocks[block]
-                    run = [item]
+                panel, place, part, w_tier, x_tier = item
+                if item in waiting and budget > 0 and panel <= highest and ready(known, *item):
+                    first, count, tiles = panels[panel]
+                    joined = [item]
                     for more in range(part + 1, count):
-                        neighbour = (block, place, more, w_tier, x_tier)
-                        if len(run) == more - part and neighbour in waiting and ready(known, *neighbour):
-                            run.append(neighbour)
-                    run = run[: 2 if len(run) == 3 else len(run)]
-                    if len(run) < min(narrowest, count) and part % 2 == 0:
+                        neighbour = (panel, place, more, w_tier, x_tier)
+                        if len(joined) == more - part and neighbour in waiting and ready(known, *neighbour):
+                            joined.append(neighbour)
+                    joined = joined[: 2 if len(joined) == 3 else len(joined)]
+                    if wide and len(joined) == 1 and count > 1 and part % 2 == 0:
                         continue
-                    width = len(run) * CHUNK
-                    opening = block not in sums
-                    if opening and block < len(blocks) - spare:
-                        sums[block] = sum_pool.tile([P, len(tiles), count * CHUNK], F32, name="sum_bank")
+                    opening = panel not in sums
+                    if opening and panel < len(panels) - late_panels:
+                        sums[panel] = sum_pool.tile([P, len(tiles), count * CHUNK], F32, name="sum_bank")
                     elif opening:
-                        sums[block] = back_pool.tile([P, len(tiles), count * CHUNK], F32, name="back_bank")
-                    for done in run:
-                        waiting.remove(done)
-                    w_columns = slice(tiles[place] * P, (tiles[place] + 1) * P)
-                    x_columns = slice((first + part) * CHUNK, (first + part) * CHUNK + width)
+                        sums[panel] = back_pool.tile([P, len(tiles), count * CHUNK], F32, name="back_bank")
+                    for written in joined:
+                        waiting.remove(written)
+                    w_columns = chunk_columns(tiles[place])
+                    x_columns = chunk_columns(first + part, len(joined))
                     nc.tensor.matmul_mx(
-                        out=sums[block][:, place, part * CHUNK : part * CHUNK + width],
+                        out=sums[panel][:, place, chunk_columns(part, len(joined))],
                         lhsT=codes["w", w_tier][:, w_columns].bitcast(FP8X4),
                         lhsT_scale=scales["w", w_tier][:, w_columns],
                         rhs=codes["x", x_tier][:, x_columns].bitcast(FP8X4),
                         rhs_scale=scales["x", x_tier][:, x_columns],
                         start=opening,
-                        stop=all(other[0] != block for other in waiting),
+                        stop=all(other[0] != panel for other in waiting),
                     )
-                    budget = budget - width
+                    budget = budget - len(joined) * CHUNK
             return budget
 
-        def finish(block):
-            first, count, tiles = blocks[block]
-            result = sb.tile([P, len(tiles), count * CHUNK], F32, name="result%d" % block, align_bytes=64)
-            together = min(TOGETHER if block >= len(blocks) - TAIL_BLOCKS else 4, len(tiles))
+        def finish(panel):
+            first, count, tiles = panels[panel]
+            result = sb.tile([P, len(tiles), count * CHUNK], F32, name="result%d" % panel, align_bytes=64)
+            together = min(STORE_TILES, len(tiles))
             for place, c in enumerate(tiles):
                 nc.scalar.activation(
-                    out=result[:, place, :], in_=sums[block][:, place, :], func=GELU, bias=bias[:, c : c + 1]
+                    out=result[:, place, :], in_=sums[panel][:, place, :], func=GELU, bias=bias[:, c : c + 1]
                 )
                 if (place + 1) % together == 0:
                     nc.sync.dma_start(
-                        out=out_rows[:, c + 1 - together : c + 1, first * CHUNK : (first + count) * CHUNK],
+                        out=out_rows[:, c + 1 - together : c + 1, chunk_columns(first, count)],
                         in_=result[:, place + 1 - together : place + 1, :],
                     )
 
-        last = len(order) - 1
-        groups = CHUNK // RUN
-        shared = list(SHARED) + [groups] * len(order)
-        early = min(GELU_AFTER, len(order))
-        for s in range(early):
-            if shared[s]:
-                round_and_interleave(order[s], slice(0, shared[s]), False)
-        late_rounds = list(range(early, len(order)))
-
-        steps = []
-        for word in STEPS.split():
-            steps.append((word[0], tuple(int(c, 16) for c in word[1:])))
-        steps = steps + [("n", (0,))] * 8
-        half = groups // 2
+        for m, chunk in enumerate(order):
+            groups = slice(0, SCALAR_GROUPS if m < SHARED_CHUNKS else GROUPS)
+            nc.scalar.copy(out=words_view(rounded_chunk(chunk, "q"))[:, groups], in_=rows_view(raw[chunk])[:, groups])
 
         brought = 0
         subtracted = 0
-        finished = [0]
+        finished = 0
         credit = 0
-        for kind, places in steps:
-            known = set(quantised)
-            if kind == "R":
-                round_and_interleave(order[places[0]], slice(shared[places[0]], groups), True)
-            elif kind == "S":
-                round_and_interleave(order[places[0]], slice(0, groups), False)
-                continue
-            elif kind == "s":
-                subtract(order[places[0]], slice(0, groups))
-                subtracted = places[0] + 1
-            elif kind == "a":
-                subtract(order[places[0]], slice(0, half))
-            elif kind == "b":
-                subtract(order[places[0]], slice(half, groups))
-                subtracted = places[0] + 1
-            elif kind != "n":
-                quantise(places, kind)
-            credit = min(credit, 0) + (PER_SUB if kind in "sn" else PER_SUB // 2 if kind in "ab" else PER_Q * len(places))
+
+        def feed_tensor(columns, known, credit, brought, finished):
+            credit = min(credit, 0) + columns
             while brought <= min(last, subtracted - 1 + BACK_AHEAD) and (order[brought][0], "q", order[brought][1]) in known:
                 bring_back(order[brought])
                 brought = brought + 1
                 credit = credit - PACK * CHUNK
-            spare = SPARE
-            highest = finished[-1] + SUM_BANKS - 1
-            limit = len(blocks) - spare - 1
-            if highest >= limit:
-                highest = limit + max(0, min(spare, subtracted - (last + 1 - BACK_BANKS)))
-            credit = multiply(credit, highest, known, 2 if subtracted >= MINW else 1, spare)
-            done = finished[-1]
-            while done < len(blocks) and all(item[0] != done for item in waiting):
-                finish(done)
-                done = done + 1
-            finished.append(done)
-        assert not waiting
+            highest = finished + SUM_BANKS - 1
+            first_late = len(panels) - late_panels
+            if highest >= first_late - 1:
+                banks_left = subtracted - (len(order) - BACK_BANKS)
+                highest = first_late - 1 + max(0, banks_left)
+            credit = multiply(credit, highest, known, subtracted >= WIDE_FROM)
+            while finished < len(panels) and all(item[0] != finished for item in waiting):
+                finish(finished)
+                finished = finished + 1
+            return credit, brought, finished
+
+        for kind, m in steps:
+            known = set(quantised)
+            if kind == "round":
+                groups = slice(SCALAR_GROUPS, GROUPS)
+                nc.vector.tensor_copy(
+                    out=words_view(rounded_chunk(order[m], "q"))[:, groups], in_=rows_view(raw[order[m]])[:, groups]
+                )
+            elif kind == "subtract":
+                subtract(order[m])
+                subtracted = m + 1
+            else:
+                quantise(order[m], kind)
+            columns = COLUMNS_PER_SUBTRACT if kind == "subtract" else COLUMNS_PER_OTHER
+            credit, brought, finished = feed_tensor(columns, known, credit, brought, finished)
+        while waiting:
+            credit, brought, finished = feed_tensor(COLUMNS_PER_SUBTRACT, quantised, credit, brought, finished)

@@ -66,17 +66,13 @@ def tile_mix_tierb_three_gelu_kernel(tc, w, x, b, out):
 
     steps = [(kind, m) for m in range(SHARED_CHUNKS) for kind in ("round", "q")]
     first_tier = SHARED_CHUNKS
-    leftover = 0
     for s in range(len(order)):
         lead = SHARED_CHUNKS if s < SHARED_CHUNKS else FIRST_TIER_AHEAD
         newest = min(last, s + lead)
-        between = [("q", m) for m in range(first_tier, newest + 1)] + [("r", m) for m in range(leftover, s)]
+        steps = steps + [("subtract", s)] + [("r", m) for m in range(max(s - 1, 0), s)]
+        steps = steps + [("q", m) for m in range(first_tier, newest + 1)]
         first_tier = newest + 1
-        leftover = s
-        if len(between) >= 2 or s == last:
-            between.append(("r", s))
-            leftover = s + 1
-        steps = steps + [("subtract", s)] + between
+    steps = steps + [("r", last)]
 
     with ExitStack() as ctx:
         sb = ctx.enter_context(tc.tile_pool(name="sb", bufs=1))

@@ -15,7 +15,6 @@ ALU = mybir.AluOpType
 GELU = mybir.ActivationFunctionType.Gelu_apprx_tanh
 
 P = 128
-BF16_ONE = 0x3F80
 PACK = 4
 CHUNK = 128
 RUN = 4
@@ -32,7 +31,8 @@ COLUMNS_PER_SUBTRACT = 1024
 COLUMNS_PER_OTHER = 256
 WIDE_FROM = 6
 STORE_TILES = 2
-TENSOR_WARM_UPS = 5
+WARM_WIDTH = 256
+TENSOR_WARM_UPS = 6
 
 
 def rows_view(rows):
@@ -98,50 +98,39 @@ def tile_mix_tierb_three_gelu_kernel(tc, w, x, b, out):
         nc.vector.memset(table_warm[:, 0:1], 0.0)
         nc.scalar.activation(out=table_warm[:, 1:2], in_=table_warm[:, 0:1], func=GELU)
 
-        ramp = sb.tile([P, K // 2], BF16, name="ramp", align_bytes=64)
-        nc.gpsimd.iota(
-            ramp[:], pattern=[[1, K // 2]], base=0, channel_multiplier=-2, allow_small_or_imprecise_dtypes=True
-        )
-        identity = sb.tile([P, PACK * K], BF16, name="identity", align_bytes=64)
+        ramp = sb.tile([P, P], BF16, name="ramp", align_bytes=64)
+        nc.gpsimd.iota(ramp[:], pattern=[[1, P]], base=0, channel_multiplier=-1, allow_small_or_imprecise_dtypes=True)
+        identity = sb.tile([P, PACK * WARM_WIDTH], BF16, name="identity", align_bytes=64)
         id_codes = sb.tile([P, K], U32, name="id_codes", align_bytes=64)
-        id_scales = sb.tile([P, K], U8, name="id_scales", align_bytes=64)
-        low_half = slice(0, K // 2)
-        high_half = slice(K // 2, K)
+        id_scales = sb.tile([P, P], U8, name="id_scales", align_bytes=64)
+        nc.vector.memset(identity[:].bitcast(I32), 0)
+        nc.vector.memset(id_codes[:, P:], 0)
 
-        def write_identity(j):
-            nc.vector.tensor_scalar(
-                out=identity[:, j * K : (j + 1) * K].bitcast(I32),
-                in0=ramp[:],
-                scalar1=float(j // 2),
-                scalar2=float(BF16_ONE << (16 * (j % 2))),
-                op0=ALU.is_equal,
-                op1=ALU.mult,
-            )
-
-        def quantise_identity(columns):
-            nc.vector.quantize_mx(
-                out=id_codes[:, columns].bitcast(FP8X4),
-                scales=id_scales[:, columns],
-                in_=identity[:, PACK * columns.start : PACK * columns.stop],
-            )
-
-        for j in range(PACK - 1):
-            write_identity(j)
-        quantise_identity(low_half)
-        write_identity(PACK - 1)
-
-        warm_bank = sum_pool.tile([P, K // 2], F32, name="sum_bank")
+        zero_codes = sb.tile([P, WARM_WIDTH], U32, name="zero_codes", align_bytes=64)
+        zero_scales = sb.tile([P, WARM_WIDTH], U8, name="zero_scales", align_bytes=64)
+        nc.vector.quantize_mx(out=zero_codes[:].bitcast(FP8X4), scales=zero_scales[:], in_=identity[:])
+        warm_bank = sum_pool.tile([P, WARM_WIDTH], F32, name="sum_bank")
         for repeat in range(TENSOR_WARM_UPS):
             nc.tensor.matmul_mx(
                 out=warm_bank[:],
-                lhsT=id_codes[:, 0:P].bitcast(FP8X4),
-                lhsT_scale=id_scales[:, 0:P],
-                rhs=id_codes[:, low_half].bitcast(FP8X4),
-                rhs_scale=id_scales[:, low_half],
+                lhsT=zero_codes[:, 0:P].bitcast(FP8X4),
+                lhsT_scale=zero_scales[:, 0:P],
+                rhs=zero_codes[:].bitcast(FP8X4),
+                rhs_scale=zero_scales[:],
                 start=True,
                 stop=True,
             )
-        quantise_identity(high_half)
+
+        first_places = identity[:, 0 : PACK * P].rearrange("p (m j) -> p m j", j=PACK)[:, :, 0]
+        nc.vector.tensor_scalar(
+            out=first_places, in0=ramp[:], scalar1=0.0, scalar2=1.0, op0=ALU.is_equal, op1=ALU.mult
+        )
+        nc.vector.quantize_mx(
+            out=id_codes[:, 0:P].bitcast(FP8X4), scales=id_scales[:], in_=identity[:, 0 : PACK * P]
+        )
+        id_bytes = id_codes[:].bitcast(U8).rearrange("p (j m t) -> p j m t", j=PACK, t=PACK)
+        for j in range(1, PACK):
+            nc.vector.tensor_copy(out=id_bytes[:, j, :, j], in_=id_bytes[:, 0, :, 0])
 
         codes = {}
         scales = {}
@@ -174,7 +163,7 @@ def tile_mix_tierb_three_gelu_kernel(tc, w, x, b, out):
                 nc.tensor.matmul_mx(
                     out=back[chunk][:, j, :],
                     lhsT=id_codes[:, j * P : (j + 1) * P].bitcast(FP8X4),
-                    lhsT_scale=id_scales[:, j * P : (j + 1) * P],
+                    lhsT_scale=id_scales[:],
                     rhs=codes[which, "q"][:, chunk_columns(i)].bitcast(FP8X4),
                     rhs_scale=scales[which, "q"][:, chunk_columns(i)],
                     start=True,

@@ -65,6 +65,7 @@ def tile_mix_tierb_three_gelu_kernel(tc, w, x, b, out):
     late_panels = len(panels) - BACK_BANKS - SUM_BANKS
 
     steps = [(kind, m) for m in range(SHARED_CHUNKS) for kind in ("round", "q")]
+    steps = steps[:1] + [("move", 1)] + steps[1:2] + [("move", j) for j in range(2, PACK)] + steps[2:]
     first_tier = SHARED_CHUNKS
     for s in range(len(order)):
         lead = SHARED_CHUNKS if s < SHARED_CHUNKS else FIRST_TIER_AHEAD
@@ -100,15 +101,16 @@ def tile_mix_tierb_three_gelu_kernel(tc, w, x, b, out):
 
         ramp = sb.tile([P, P], BF16, name="ramp", align_bytes=64)
         nc.gpsimd.iota(ramp[:], pattern=[[1, P]], base=0, channel_multiplier=-1, allow_small_or_imprecise_dtypes=True)
-        identity = sb.tile([P, PACK * WARM_WIDTH], BF16, name="identity", align_bytes=64)
-        id_codes = sb.tile([P, K], U32, name="id_codes", align_bytes=64)
+        identity = sb.tile([P, PACK * P], BF16, name="identity", align_bytes=64)
+        id_words = sb.tile([P, K + P], U32, name="id_codes", align_bytes=64)
+        id_codes = id_words[:, 0:K]
         id_scales = sb.tile([P, P], U8, name="id_scales", align_bytes=64)
+        nc.vector.memset(id_words[:, P:], 0)
         nc.vector.memset(identity[:].bitcast(I32), 0)
-        nc.vector.memset(id_codes[:, P:], 0)
 
         zero_codes = sb.tile([P, WARM_WIDTH], U32, name="zero_codes", align_bytes=64)
         zero_scales = sb.tile([P, WARM_WIDTH], U8, name="zero_scales", align_bytes=64)
-        nc.vector.quantize_mx(out=zero_codes[:].bitcast(FP8X4), scales=zero_scales[:], in_=identity[:])
+        nc.vector.quantize_mx(out=zero_codes[:].bitcast(FP8X4), scales=zero_scales[:], in_=id_words[:, P:].bitcast(BF16))
         warm_bank = sum_pool.tile([P, WARM_WIDTH], F32, name="sum_bank")
         for repeat in range(TENSOR_WARM_UPS):
             nc.tensor.matmul_mx(
@@ -121,15 +123,14 @@ def tile_mix_tierb_three_gelu_kernel(tc, w, x, b, out):
                 stop=True,
             )
 
-        first_places = identity[:, 0 : PACK * P].rearrange("p (m j) -> p m j", j=PACK)[:, :, 0]
+        first_places = identity[:].rearrange("p (m j) -> p m j", j=PACK)[:, :, 0]
         nc.vector.tensor_scalar(
             out=first_places, in0=ramp[:], scalar1=0.0, scalar2=1.0, op0=ALU.is_equal, op1=ALU.mult
         )
-        nc.vector.quantize_mx(
-            out=id_codes[:, 0:P].bitcast(FP8X4), scales=id_scales[:], in_=identity[:, 0 : PACK * P]
-        )
-        id_bytes = id_codes[:].bitcast(U8).rearrange("p (j m t) -> p j m t", j=PACK, t=PACK)
-        for j in range(1, PACK):
+        nc.vector.quantize_mx(out=id_codes[:, 0:P].bitcast(FP8X4), scales=id_scales[:], in_=identity[:])
+        id_bytes = id_codes.bitcast(U8).rearrange("p (j m t) -> p j m t", j=PACK, t=PACK)
+
+        def move_identity_bytes(j):
             nc.vector.tensor_copy(out=id_bytes[:, j, :, j], in_=id_bytes[:, 0, :, 0])
 
         codes = {}
@@ -273,6 +274,10 @@ def tile_mix_tierb_three_gelu_kernel(tc, w, x, b, out):
                 nc.vector.tensor_copy(
                     out=words_view(rounded_chunk(order[m], "q"))[:, groups], in_=rows_view(raw[order[m]])[:, groups]
                 )
+            elif kind == "move":
+                move_identity_bytes(m)
+                if m < PACK - 1:
+                    continue
             elif kind == "subtract":
                 subtract(order[m])
                 subtracted = m + 1

@@ -21,8 +21,8 @@ RUN = 4
 GROUPS = CHUNK // RUN
 
 SINGLE_LOADS = 8
-SHARED_CHUNKS = 2
-SCALAR_GROUPS = 10
+SCALAR_GROUPS = (10, 10, 16)
+EARLY_CHUNKS = 2
 FIRST_TIER_AHEAD = 3
 BACK_BANKS = 3
 SUM_BANKS = 5
@@ -64,11 +64,11 @@ def tile_mix_tierb_three_gelu_kernel(tc, w, x, b, out):
     panels = panels + [(3 * quarter, quarter, (c,)) for c in range(n_tiles)]
     late_panels = len(panels) - BACK_BANKS - SUM_BANKS
 
-    steps = [(kind, m) for m in range(SHARED_CHUNKS) for kind in ("round", "q")]
-    steps = steps[:1] + [("move", 1)] + steps[1:2] + [("move", j) for j in range(2, PACK)] + steps[2:]
-    first_tier = SHARED_CHUNKS
+    steps = [(kind, m) for m in range(EARLY_CHUNKS) for kind in ("round", "q")]
+    steps = steps + [("round", m) for m in range(EARLY_CHUNKS, len(SCALAR_GROUPS))]
+    first_tier = EARLY_CHUNKS
     for s in range(len(order)):
-        lead = SHARED_CHUNKS if s < SHARED_CHUNKS else FIRST_TIER_AHEAD
+        lead = EARLY_CHUNKS if s < EARLY_CHUNKS else FIRST_TIER_AHEAD
         newest = min(last, s + lead)
         steps = steps + [("subtract", s)] + [("r", m) for m in range(max(s - 1, 0), s)]
         steps = steps + [("q", m) for m in range(first_tier, newest + 1)]
@@ -129,8 +129,7 @@ def tile_mix_tierb_three_gelu_kernel(tc, w, x, b, out):
         )
         nc.vector.quantize_mx(out=id_codes[:, 0:P].bitcast(FP8X4), scales=id_scales[:], in_=identity[:])
         id_bytes = id_codes.bitcast(U8).rearrange("p (j m t) -> p j m t", j=PACK, t=PACK)
-
-        def move_identity_bytes(j):
+        for j in range(1, PACK):
             nc.vector.tensor_copy(out=id_bytes[:, j, :, j], in_=id_bytes[:, 0, :, 0])
 
         codes = {}
@@ -242,7 +241,7 @@ def tile_mix_tierb_three_gelu_kernel(tc, w, x, b, out):
                     )
 
         for m, chunk in enumerate(order):
-            groups = slice(0, SCALAR_GROUPS if m < SHARED_CHUNKS else GROUPS)
+            groups = slice(0, SCALAR_GROUPS[m] if m < len(SCALAR_GROUPS) else GROUPS)
             nc.scalar.copy(out=words_view(rounded_chunk(chunk, "q"))[:, groups], in_=rows_view(raw[chunk])[:, groups])
 
         brought = 0
@@ -270,14 +269,10 @@ def tile_mix_tierb_three_gelu_kernel(tc, w, x, b, out):
         for kind, m in steps:
             known = set(quantised)
             if kind == "round":
-                groups = slice(SCALAR_GROUPS, GROUPS)
+                groups = slice(SCALAR_GROUPS[m], GROUPS)
                 nc.vector.tensor_copy(
                     out=words_view(rounded_chunk(order[m], "q"))[:, groups], in_=rows_view(raw[order[m]])[:, groups]
                 )
-            elif kind == "move":
-                move_identity_bytes(m)
-                if m < PACK - 1:
-                    continue
             elif kind == "subtract":
                 subtract(order[m])
                 subtracted = m + 1

@@ -70,8 +70,10 @@ def tile_mix_tierb_three_gelu_kernel(tc, w, x, b, out):
     for s in range(len(order)):
         lead = EARLY_CHUNKS if s < EARLY_CHUNKS else FIRST_TIER_AHEAD
         newest = min(last, s + lead)
-        steps = steps + [("subtract", s)] + [("r", m) for m in range(max(s - 1, 0), s)]
-        steps = steps + [("q", m) for m in range(first_tier, newest + 1)]
+        steps = steps + [("subtract", s)] + [("r", m) for m in range(max(s - 1, 0), s) if ("r", m) not in steps]
+        steps = steps + [("q", m) for m in range(first_tier, newest)]
+        steps = steps + [("r", m) for m in range(s, s + newest - first_tier)]
+        steps = steps + [("q", m) for m in range(max(first_tier, newest), newest + 1)]
         first_tier = newest + 1
     steps = steps + [("r", last)]
 

@@ -20,8 +20,8 @@ CHUNK = 128
 RUN = 4
 GROUPS = CHUNK // RUN
 
-SINGLE_LOADS = 8
-SCALAR_GROUPS = (10, 10, 16)
+SINGLE_LOADS = 10
+SCALAR_GROUPS = (10, 10)
 EARLY_CHUNKS = 2
 FIRST_TIER_AHEAD = 3
 BACK_BANKS = 3

from contextlib import ExitStack

import concourse.mybir as mybir

K, N, T = 512, 512, 1024
FLOPS = 3 * 2 * K * N * T

F32 = mybir.dt.float32
BF16 = mybir.dt.bfloat16
U32 = mybir.dt.uint32
I32 = mybir.dt.int32
U8 = mybir.dt.uint8
FP8X4 = mybir.dt.float8_e4m3fn_x4
ALU = mybir.AluOpType
GELU = mybir.ActivationFunctionType.Gelu_apprx_tanh

P = 128
PACK = 4
CHUNK = 128
RUN = 4
GROUPS = CHUNK // RUN

SINGLE_LOADS = 10
SCALAR_GROUPS = (10, 10)
EARLY_CHUNKS = 2
FIRST_TIER_AHEAD = 3
BACK_BANKS = 3
SUM_BANKS = 5
BACK_AHEAD = BACK_BANKS - 1
COLUMNS_PER_SUBTRACT = 1024
COLUMNS_PER_OTHER = 256
WIDE_FROM = 6
STORE_TILES = 2
WARM_WIDTH = 256
TENSOR_WARM_UPS = 6


def rows_view(rows):
    return rows.rearrange("p j (g i) -> p g j i", i=RUN)


def words_view(interleaved):
    return interleaved.rearrange("p (g i j) -> p g j i", i=RUN, j=PACK)


def chunk_columns(index, count=1):
    return slice(index * CHUNK, (index + count) * CHUNK)


def tile_mix_tierb_three_gelu_kernel(tc, w, x, b, out):
    nc = tc.nc
    n_tiles = N // P
    quarter = T // CHUNK // 4

    order = [(which, i) for i in range(quarter) for which in ("w", "x")]
    order = order + [("x", i) for i in range(quarter, 2 * quarter)]
    order = order + [("w", i) for i in range(quarter, n_tiles)]
    order = order + [("x", i) for i in range(2 * quarter, 4 * quarter)]
    last = len(order) - 1

    panels = [(q * quarter, quarter, tuple(range(quarter))) for q in range(2)]
    panels = panels + [(0, 2 * quarter, (c,)) for c in range(quarter, n_tiles)]
    panels = panels + [(i, 1, tuple(range(n_tiles))) for i in range(2 * quarter, 3 * quarter)]
    panels = panels + [(3 * quarter, quarter, (c,)) for c in range(n_tiles)]
    late_panels = len(panels) - BACK_BANKS - SUM_BANKS

    steps = [(kind, m) for m in range(EARLY_CHUNKS) for kind in ("round", "q")]
    steps = steps + [("round", m) for m in range(EARLY_CHUNKS, len(SCALAR_GROUPS))]
    first_tier = EARLY_CHUNKS
    for s in range(len(order)):
        lead = EARLY_CHUNKS if s < EARLY_CHUNKS else FIRST_TIER_AHEAD
        newest = min(last, s + lead)
        steps = steps + [("subtract", s)] + [("r", m) for m in range(max(s - 1, 0), s) if ("r", m) not in steps]
        steps = steps + [("q", m) for m in range(first_tier, newest)]
        steps = steps + [("r", m) for m in range(s, s + newest - first_tier)]
        steps = steps + [("q", m) for m in range(max(first_tier, newest), newest + 1)]
        first_tier = newest + 1
    steps = steps + [("r", last)]

    with ExitStack() as ctx:
        sb = ctx.enter_context(tc.tile_pool(name="sb", bufs=1))
        back_pool = ctx.enter_context(tc.psum_pool(name="back", bufs=BACK_BANKS))
        sum_pool = ctx.enter_context(tc.psum_pool(name="sums", bufs=SUM_BANKS))
        ctx.enter_context(tc.manual_schedule())

        matrix = {"w": w, "x": x}
        raw = {}
        bias = sb.tile([P, n_tiles], F32, name="bias", align_bytes=64)
        for place in list(range(SINGLE_LOADS)) + list(range(SINGLE_LOADS, len(order), 2)):
            which, first = order[place]
            count = 1 if place < SINGLE_LOADS else 2
            landed = sb.tile([P, PACK, count * CHUNK], F32, name="raw_%s%d" % (which, first), align_bytes=64)
            rows = matrix[which][:, chunk_columns(first, count)].rearrange("(p j) c -> p j c", j=PACK)
            nc.sync.dma_start(out=landed[:], in_=rows)
            for i in range(count):
                raw[which, first + i] = landed[:, :, chunk_columns(i)]
        with nc.allow_non_contiguous_dma(reason="one bias value for each partition and n tile"):
            nc.sync.dma_start(out=bias[:], in_=b.rearrange("(c p) -> p c", p=P))

        table_warm = sb.tile([P, 2], F32, name="table_warm", align_bytes=64)
        nc.vector.memset(table_warm[:, 0:1], 0.0)
        nc.scalar.activation(out=table_warm[:, 1:2], in_=table_warm[:, 0:1], func=GELU)

        ramp = sb.tile([P, P], BF16, name="ramp", align_bytes=64)
        nc.gpsimd.iota(ramp[:], pattern=[[1, P]], base=0, channel_multiplier=-1, allow_small_or_imprecise_dtypes=True)
        identity = sb.tile([P, PACK * P], BF16, name="identity", align_bytes=64)
        id_words = sb.tile([P, K + P], U32, name="id_codes", align_bytes=64)
        id_codes = id_words[:, 0:K]
        id_scales = sb.tile([P, P], U8, name="id_scales", align_bytes=64)
        nc.vector.memset(id_words[:, P:], 0)
        nc.vector.memset(identity[:].bitcast(I32), 0)

        zero_codes = sb.tile([P, WARM_WIDTH], U32, name="zero_codes", align_bytes=64)
        zero_scales = sb.tile([P, WARM_WIDTH], U8, name="zero_scales", align_bytes=64)
        nc.vector.quantize_mx(out=zero_codes[:].bitcast(FP8X4), scales=zero_scales[:], in_=id_words[:, P:].bitcast(BF16))
        warm_bank = sum_pool.tile([P, WARM_WIDTH], F32, name="sum_bank")
        for repeat in range(TENSOR_WARM_UPS):
            nc.tensor.matmul_mx(
                out=warm_bank[:],
                lhsT=zero_codes[:, 0:P].bitcast(FP8X4),
                lhsT_scale=zero_scales[:, 0:P],
                rhs=zero_codes[:].bitcast(FP8X4),
                rhs_scale=zero_scales[:],
                start=True,
                stop=True,
            )

        first_places = identity[:].rearrange("p (m j) -> p m j", j=PACK)[:, :, 0]
        nc.vector.tensor_scalar(
            out=first_places, in0=ramp[:], scalar1=0.0, scalar2=1.0, op0=ALU.is_equal, op1=ALU.mult
        )
        nc.vector.quantize_mx(out=id_codes[:, 0:P].bitcast(FP8X4), scales=id_scales[:], in_=identity[:])
        id_bytes = id_codes.bitcast(U8).rearrange("p (j m t) -> p j m t", j=PACK, t=PACK)
        for j in range(1, PACK):
            nc.vector.tensor_copy(out=id_bytes[:, j, :, j], in_=id_bytes[:, 0, :, 0])

        codes = {}
        scales = {}
        rounded = {}
        for which, width in (("w", N), ("x", T)):
            for tier in ("q", "r"):
                codes[which, tier] = sb.tile([P, width], U32, name="codes_" + which + tier, align_bytes=64)
                scales[which, tier] = sb.tile([P, width], U8, name="scales_" + which + tier, align_bytes=64)
                rounded[which, tier] = sb.tile([P, PACK * width], BF16, name="bf_" + which + tier, align_bytes=64)
        quantised = set()
        back = {}

        def rounded_chunk(chunk, tier):
            which, i = chunk
            return rounded[which, tier][:, i * CHUNK * PACK : (i + 1) * CHUNK * PACK]

        def quantise(chunk, tier):
            which, i = chunk
            nc.vector.quantize_mx(
                out=codes[which, tier][:, chunk_columns(i)].bitcast(FP8X4),
                scales=scales[which, tier][:, chunk_columns(i)],
                in_=rounded_chunk(chunk, tier),
            )
            quantised.add((which, tier, i))

        def bring_back(chunk):
            which, i = chunk
            back[chunk] = back_pool.tile([P, PACK, CHUNK], F32, name="back_bank")
            for j in range(PACK):
                nc.tensor.matmul_mx(
                    out=back[chunk][:, j, :],
                    lhsT=id_codes[:, j * P : (j + 1) * P].bitcast(FP8X4),
                    lhsT_scale=id_scales[:],
                    rhs=codes[which, "q"][:, chunk_columns(i)].bitcast(FP8X4),
                    rhs_scale=scales[which, "q"][:, chunk_columns(i)],
                    start=True,
                    stop=True,
                )

        def subtract(chunk):
            nc.vector.tensor_tensor(
                out=words_view(rounded_chunk(chunk, "r")),
                in0=rows_view(raw[chunk]),
                in1=rows_view(back[chunk][:]),
                op=ALU.subtract,
            )

        waiting = [
            (panel, place, part, w_tier, x_tier)
            for panel, (first, count, tiles) in enumerate(panels)
            for w_tier, x_tier in (("q", "q"), ("r", "q"), ("q", "r"))
            for place in range(len(tiles))
            for part in range(count)
        ]
        sums = {}
        out_rows = out.rearrange("(c p) t -> p c t", p=P)

        def ready(known, panel, place, part, w_tier, x_tier):
            first, count, tiles = panels[panel]
            return ("w", w_tier, tiles[place]) in known and ("x", x_tier, first + part) in known

        def multiply(budget, highest, known, wide):
            for item in list(waiting):
                panel, place, part, w_tier, x_tier = item
                if item in waiting and budget > 0 and panel <= highest and ready(known, *item):
                    first, count, tiles = panels[panel]
                    joined = [item]
                    for more in range(part + 1, count):
                        neighbour = (panel, place, more, w_tier, x_tier)
                        if len(joined) == more - part and neighbour in waiting and ready(known, *neighbour):
                            joined.append(neighbour)
                    joined = joined[: 2 if len(joined) == 3 else len(joined)]
                    if wide and len(joined) == 1 and count > 1 and part % 2 == 0:
                        continue
                    opening = panel not in sums
                    if opening and panel < len(panels) - late_panels:
                        sums[panel] = sum_pool.tile([P, len(tiles), count * CHUNK], F32, name="sum_bank")
                    elif opening:
                        sums[panel] = back_pool.tile([P, len(tiles), count * CHUNK], F32, name="back_bank")
                    for written in joined:
                        waiting.remove(written)
                    w_columns = chunk_columns(tiles[place])
                    x_columns = chunk_columns(first + part, len(joined))
                    nc.tensor.matmul_mx(
                        out=sums[panel][:, place, chunk_columns(part, len(joined))],
                        lhsT=codes["w", w_tier][:, w_columns].bitcast(FP8X4),
                        lhsT_scale=scales["w", w_tier][:, w_columns],
                        rhs=codes["x", x_tier][:, x_columns].bitcast(FP8X4),
                        rhs_scale=scales["x", x_tier][:, x_columns],
                        start=opening,
                        stop=all(other[0] != panel for other in waiting),
                    )
                    budget = budget - len(joined) * CHUNK
            return budget

        def finish(panel):
            first, count, tiles = panels[panel]
            result = sb.tile([P, len(tiles), count * CHUNK], F32, name="result%d" % panel, align_bytes=64)
            together = min(STORE_TILES, len(tiles))
            for place, c in enumerate(tiles):
                nc.scalar.activation(
                    out=result[:, place, :], in_=sums[panel][:, place, :], func=GELU, bias=bias[:, c : c + 1]
                )
                if (place + 1) % together == 0:
                    nc.sync.dma_start(
                        out=out_rows[:, c + 1 - together : c + 1, chunk_columns(first, count)],
                        in_=result[:, place + 1 - together : place + 1, :],
                    )

        for m, chunk in enumerate(order):
            groups = slice(0, SCALAR_GROUPS[m] if m < len(SCALAR_GROUPS) else GROUPS)
            nc.scalar.copy(out=words_view(rounded_chunk(chunk, "q"))[:, groups], in_=rows_view(raw[chunk])[:, groups])

        brought = 0
        subtracted = 0
        finished = 0
        credit = 0

        def feed_tensor(columns, known, credit, brought, finished):
            credit = min(credit, 0) + columns
            while brought <= min(last, subtracted - 1 + BACK_AHEAD) and (order[brought][0], "q", order[brought][1]) in known:
                bring_back(order[brought])
                brought = brought + 1
                credit = credit - PACK * CHUNK
            highest = finished + SUM_BANKS - 1
            first_late = len(panels) - late_panels
            if highest >= first_late - 1:
                banks_left = subtracted - (len(order) - BACK_BANKS)
                highest = first_late - 1 + max(0, banks_left)
            credit = multiply(credit, highest, known, subtracted >= WIDE_FROM)
            while finished < len(panels) and all(item[0] != finished for item in waiting):
                finish(finished)
                finished = finished + 1
            return credit, brought, finished

        for kind, m in steps:
            known = set(quantised)
            if kind == "round":
                groups = slice(SCALAR_GROUPS[m], GROUPS)
                nc.vector.tensor_copy(
                    out=words_view(rounded_chunk(order[m], "q"))[:, groups], in_=rows_view(raw[order[m]])[:, groups]
                )
            elif kind == "subtract":
                subtract(order[m])
                subtracted = m + 1
            else:
                quantise(order[m], kind)
            columns = COLUMNS_PER_SUBTRACT if kind == "subtract" else COLUMNS_PER_OTHER
            credit, brought, finished = feed_tensor(columns, known, credit, brought, finished)
        while waiting:
            credit, brought, finished = feed_tensor(COLUMNS_PER_SUBTRACT, quantised, credit, brought, finished)
